import numpy as np
import ml_dtypes


def mxq(x, axis, fmt="e4m3"):
    dtype, down = {"e4m3": (ml_dtypes.float8_e4m3fn, 7), "e5m2": (ml_dtypes.float8_e5m2, 14)}[fmt]
    v = np.moveaxis(np.asarray(x, np.float32).astype(ml_dtypes.bfloat16).astype(np.float64), axis, -1)
    blocks = v.reshape(v.shape[:-1] + (-1, 32))
    amax = np.abs(blocks).max(-1, keepdims=True)
    byte = np.maximum(np.where(amax > 0, np.frexp(amax)[1] - 1 + 127, 0) - down, 1)
    scale = np.exp2(byte - 127.0)
    codes = (blocks / scale).astype(np.float32).astype(dtype).astype(np.float64)
    return np.moveaxis((codes * scale).reshape(v.shape), -1, axis)


WIDE = False


def mx_kscale(k):
    if not WIDE:
        return np.ones(k)
    levels = np.array([10, -10, 5, -5, 0])
    if k % 512:
        return np.exp2(np.random.permutation(np.resize(levels, k // 32))).repeat(32)
    a = np.empty((k // 512, 16))
    for p in range(k // 512):
        a[p, :8] = np.random.permutation(np.resize(levels, 8))
        for g in range(8):
            far = levels[np.abs(levels - a[p, g]) >= 10]
            a[p, g + 8] = far[np.random.randint(len(far))]
    return np.exp2(a.ravel()).repeat(32)


BF16 = ml_dtypes.bfloat16


def bf(x):
    return np.asarray(x, np.float32).astype(BF16)


def f64(x):
    return np.asarray(x).astype(np.float64)


E2M1 = np.array([0.0, 0.5, 1.0, 1.5, 2.0, 3.0, 4.0, 6.0, -0.0, -0.5, -1.0, -1.5, -2.0, -3.0, -4.0, -6.0])


def pack_weight(w, fmt):
    k, n = w.shape
    w = f64(bf(w)).reshape(k // 32, 32, n)
    amax = np.abs(w).max(1)
    if fmt == "e4m3":
        byte = np.frexp(amax)[1] - 1 + 127 - 7
    else:
        mant, ex = np.frexp(amax / 6.0)
        byte = np.where(mant > 0.5, ex, ex - 1) + 127
    byte = np.clip(np.where(amax > 0, byte, 1), 1, 254)
    scaled = (w * np.exp2(127.0 - byte)[:, None, :]).reshape(k, n).astype(np.float32)
    by_word = np.ascontiguousarray(scaled.reshape(k // 512, 128, 4, n).transpose(0, 1, 3, 2))
    if fmt == "e4m3":
        words = by_word.astype(ml_dtypes.float8_e4m3fn).view(np.uint8)
    else:
        c = by_word.astype(ml_dtypes.float4_e2m1fn).view(np.uint8) & 0xF
        words = c[..., 0::2] | (c[..., 1::2] << 4)
    return np.ascontiguousarray(words), np.ascontiguousarray(byte.astype(np.uint8).reshape(k // 512, 16, n))


def unpack_weight(words, scales, fmt):
    g, p, n, _ = words.shape
    if fmt == "e4m3":
        vals = np.ascontiguousarray(words).view(ml_dtypes.float8_e4m3fn).astype(np.float64)
    else:
        nib = np.empty((g, p, n, 4), np.uint8)
        nib[..., 0::2] = words & 0xF
        nib[..., 1::2] = words >> 4
        vals = E2M1[nib]
    vals = vals * np.repeat(np.exp2(scales.astype(np.float64) - 127.0), 8, axis=1)[..., None]
    return vals.transpose(0, 1, 3, 2).reshape(g * 512, n)
def pack4(w):
    words, scales = pack_weight(w, "e2m1")
    return words.reshape(words.shape[0], 128, -1), scales


def unpack4(words, scales):
    return unpack_weight(words.reshape(words.shape[0], 128, -1, 2), scales, "e2m1")


def planes(Y):
    n, m = Y.shape
    b = f64(bf(Y)).reshape(n // 32, 32, m)
    amax = np.abs(b).max(1)
    byte = np.clip(np.where(amax > 0, np.frexp(amax)[1] - 1 + 127 - 7, 1), 1, 254)
    codes = (b * np.exp2(127.0 - byte)[:, None, :]).reshape(n, m).astype(np.float32).astype(ml_dtypes.float8_e4m3fn).view(np.uint8)
    words = codes.reshape(n // 512, 128, 4, m).transpose(0, 1, 3, 2)
    return np.ascontiguousarray(words), np.ascontiguousarray(byte.astype(np.uint8).reshape(n // 512, 16, m))


M, C, D, F, N = 1024, 2048, 512, 1024, 1536
MIN_D2 = 1e-4

def setup_inputs():
    rn = np.random.randn
    sc, sd, sf = mx_kscale(C), mx_kscale(D), mx_kscale(F)
    px, py = np.random.uniform(-1, 1, M), np.random.uniform(-1, 1, M)
    cx, cy = np.random.uniform(-1, 1, C), np.random.uniform(-1, 1, C)
    d2 = (px[:, None] - cx[None, :]) ** 2 + (py[:, None] - cy[None, :]) ** 2
    w_words, w_scales = pack4(0.5 * rn(C, F) / np.sqrt(C) / sc[:, None])
    return {
        "d2": bf(np.maximum(d2, MIN_D2)),
        "influence": bf(np.exp(0.3 * rn(C)) * sc),
        "w_words": w_words, "w_scales": w_scales,
        "x": bf(rn(M, D) * sd[None, :]),
        "a": bf(0.7 * rn(D, F) / np.sqrt(D) / sd[:, None]),
        "amp": bf(np.exp(0.3 * rn(F)) * sf),
        "v": bf(1.5 * rn(F, N) / np.sqrt(F) / sf[:, None]),
        "bias": bf(0.3 * rn(N)),
        "base": bf(0.5 * rn(M, N)),
        "spread": bf(np.exp(0.8 * rn(N))),
    }

def reference(d2, influence, w_words, w_scales, x, a, amp, v, bias, base, spread):
    r2 = f64(d2)
    U = r2 * np.log(r2) * f64(influence)
    W = unpack4(w_words, w_scales)
    S = (mxq(U, 1) @ W) + (mxq(f64(x), 1) @ mxq(f64(a), 0))
    H = np.tanh(S) * f64(amp)
    y = ((mxq(H, 1) @ mxq(f64(v), 0)) + f64(bias) + f64(base)) * f64(spread)
    Y = y.T
    words, scales = planes(Y)
    return y, words, scales

@@ -1,0 +1,510 @@
+from contextlib import ExitStack
+
+import concourse.mybir as mybir
+from concourse.masks import make_identity
+
+M, C, D, F, N = 1024, 2048, 512, 1024, 1536
+FLOPS = 2 * M * C * F + 2 * M * D * F + 2 * M * F * N
+
+F32 = mybir.dt.float32
+BF16 = mybir.dt.bfloat16
+U32 = mybir.dt.uint32
+I32 = mybir.dt.int32
+U8 = mybir.dt.uint8
+FP8X4 = mybir.dt.float8_e4m3fn_x4
+FP4X4 = mybir.dt.float4_e2m1fn_x4
+ACT = mybir.ActivationFunctionType
+ALU = mybir.AluOpType
+
+P = 128
+PACK = 4
+KP = 512
+MB = 512
+U_SPLIT = [256, 224, 224, 224, 224, 224, 0]
+MAIN_BUFS = 2
+UNITS = [(0, 0), (0, 1), (0, 2), (1, 0), (1, 1), (1, 2)]
+
+
+def tile_thin_plate_kernel_warp_k6_kernel(
+    tc, d2, influence, w_words, w_scales, x, a, amp, v, bias, base, spread, out_0, out_1, out_2
+):
+    nc = tc.nc
+    with ExitStack() as ctx:
+        keep = ctx.enter_context(tc.tile_pool(name="keep", bufs=1))
+        work = ctx.enter_context(tc.tile_pool(name="work", bufs=2))
+        psum = ctx.enter_context(tc.psum_pool(name="psum", bufs=1))
+        ctx.enter_context(tc.manual_schedule())
+
+        t_ = {}
+
+        def bank(i):
+            return psum.tile([P, 512], F32, name="bank%d" % i, tag="bank%d" % i)
+
+        def raw_tile(shape, dtype):
+            return work.tile(shape, dtype, name="raw", tag="raw", bufs=12, align_bytes=64)
+
+        def codes_tiles(name):
+            codes = keep.tile([P, 512], U32, name=name + "_codes", align_bytes=64)
+            scales = keep.tile([P, 512], U8, name=name + "_scales", align_bytes=64)
+            return codes, scales
+
+        def grouped_tile(tag="grouped", bufs=3):
+            return work.tile([P, 512, PACK], BF16, name=tag, tag=tag, bufs=bufs, align_bytes=64)
+
+        def quantize(key, name):
+            codes, scales = codes_tiles(name)
+            nc.vector.quantize_mx(
+                out=codes[:].bitcast(FP8X4), scales=scales[:], in_=t_["grouped", key][:].rearrange("p m t -> p (m t)")
+            )
+            t_["mx", key] = (codes, scales)
+
+        def engine_copy(on_scalar, out, in_):
+            if on_scalar:
+                nc.scalar.copy(out=out, in_=in_)
+            else:
+                nc.vector.tensor_copy(out=out, in_=in_)
+
+        def load_rows(key, src, b, g):
+            raw = raw_tile([P, PACK, 512], BF16)
+            view = src[b * MB : (b + 1) * MB, g * 512 : (g + 1) * 512].rearrange("(i p) c -> p i c", p=P)
+            nc.sync.dma_start(out=raw[:], in_=view)
+            t_["raw", key] = raw
+
+        def load_a(h):
+            raw = raw_tile([P, PACK, 512], BF16)
+            nc.sync.dma_start(out=raw[:], in_=a[:, h * 512 : (h + 1) * 512].rearrange("(p j) f -> p j f", j=PACK))
+            t_["raw", ("a", h)] = raw
+
+        def load_w(pair):
+            raw = raw_tile([P, 2, 2048], U8)
+            nc.sync.dma_start(
+                out=raw[:].bitcast(I32), in_=w_words[2 * pair : 2 * pair + 2].rearrange("g p n -> p g n").bitcast(I32)
+            )
+            t_["raw", ("w", pair)] = raw
+
+        def clear_w_scales():
+            raw = raw_tile([P, 4, 1024], U8)
+            nc.gpsimd.memset(raw[:].bitcast(I32), 0)
+            t_["raw", "ws"] = raw
+
+        def load_w_scales():
+            raw = t_["raw", "ws"]
+            for q in range(4):
+                nc.sync.dma_start(
+                    out=raw[32 * q : 32 * q + 4].bitcast(I32),
+                    in_=w_scales[:, 4 * q : 4 * q + 4, :].rearrange("g r n -> r g n").bitcast(I32),
+                )
+
+        def load_v(h):
+            raw = keep.tile([P, PACK, N], BF16, name="v_raw%d" % h)
+            rows = v[h * 512 : (h + 1) * 512, :].rearrange("(q t e) n -> e q t n", t=PACK, e=4)
+            for e in range(4):
+                nc.sync.dma_start(out=raw[e:P:4], in_=rows[e])
+            t_["raw", ("v", h)] = raw
+
+        def load_columns(name, vec, groups):
+            cols = keep.tile([P, groups, PACK], BF16, name=name)
+            nc.sync.dma_start(out=cols[:], in_=vec.rearrange("(g p t) -> p g t", p=P, t=PACK))
+            t_[name] = cols
+
+        def load_amp():
+            rows = keep.tile([8, P], BF16, name="amp_rows")
+            for h in range(2):
+                nc.sync.dma_start(
+                    out=rows[4 * h : 4 * h + 4].rearrange("t (q e) -> t q e", e=4),
+                    in_=amp[h * 512 : (h + 1) * 512].rearrange("(q t e) -> t q e", t=PACK, e=4),
+                )
+            t_["amp_rows"] = rows
+
+        ident = keep.tile([P, P], F32, name="ident")
+        amp_wide = keep.tile([P, P], F32, name="amp_wide")
+        amp_cols = keep.tile([P, 8], F32, name="amp_cols")
+        spread_cols = keep.tile([P, 3, PACK], F32, name="spread_cols")
+        shift_cols = keep.tile([P, 3, PACK], F32, name="shift_cols")
+        w_codes = keep.tile([P, 4, 2, PACK, 256], U8, name="w_codes", align_bytes=64)
+        w_plane = keep.tile([P, 4, 2, PACK, 128], U8, name="w_plane", align_bytes=64)
+        y_plane0 = keep.tile([P, 3, MB], U8, name="y_plane0", align_bytes=64)
+        y_plane1 = keep.tile([P, 3, MB], U8, name="y_plane1", align_bytes=64)
+        y_planes = [y_plane0, y_plane1]
+        warm = keep.tile([P, 2], F32, name="warm")
+
+        def amp_widen():
+            nc.vector.tensor_copy(out=amp_wide[0:8], in_=t_["amp_rows"][:])
+
+        def amp_turn(i):
+            t_["amp_bank"] = bank(i)
+            nc.tensor.transpose(t_["amp_bank"][:, 0:P], amp_wide[:], ident[:])
+
+        def amp_take():
+            nc.vector.tensor_copy(out=amp_cols[:], in_=t_["amp_bank"][:, 0:8])
+
+        def channel_constants():
+            nc.vector.tensor_copy(out=spread_cols[:], in_=t_["spread_bf"][:])
+            nc.vector.tensor_tensor(out=shift_cols[:], in0=t_["bias_bf"][:], in1=t_["spread_bf"][:], op=ALU.mult)
+
+        def deal_w(pair):
+            src = t_["raw", ("w", pair)][:].bitcast(I32).rearrange("p g (h q t w) -> p (g h) t q w", h=2, t=PACK, w=2)
+            dst = w_codes[:, 2 * pair : 2 * pair + 2].bitcast(I32).rearrange("p g h t (q w) -> p (g h) t q w", w=2)
+            nc.vector.tensor_copy(out=dst, in_=src)
+
+        def deal_w_scales():
+            src = t_["raw", "ws"][:].bitcast(I32).rearrange("p g (h q t) -> p (g h) q t", h=2, t=PACK)
+            dst = w_plane[:].bitcast(I32).rearrange("p g h t q -> p (g h) q t")
+            nc.vector.tensor_copy(out=dst, in_=src)
+
+        def turn_pairs(key, u, i):
+            words = t_["raw", key][:].bitcast(F32)
+            bk = bank(i)
+            for r in range(4):
+                nc.tensor.transpose(bk[:, r * P : (r + 1) * P], words[:, r, u:256:2], ident[:])
+            t_["bank", key, u] = bk
+
+        def pair_half(key, t):
+            return t_["bank", key, t // 2][:].bitcast(BF16)[:, t % 2 : 1024 : 2]
+
+        def turn_x(b, half, i):
+            words = t_["raw", ("x", b)][:].bitcast(F32)
+            bk = bank(i)
+            for r in range(2):
+                for u in range(2):
+                    col = (2 * r + u) * P
+                    nc.tensor.transpose(bk[:, col : col + P], words[:, 2 * half + r, u:256:2], ident[:])
+            t_["bank", ("x", b), half] = bk
+
+        def take_x(b, half):
+            if half == 0:
+                t_["grouped", ("x", b)] = grouped_tile()
+            words = t_["grouped", ("x", b)][:].rearrange("p m t -> p (m t)").bitcast(F32)
+            nc.scalar.copy(
+                out=words[:, half * 512 : (half + 1) * 512].rearrange("p (r m u) -> p r m u", r=2, u=2),
+                in_=t_["bank", ("x", b), half][:].rearrange("p (r u m) -> p r m u", r=2, u=2),
+            )
+
+        def log_d2(k, u):
+            if u == 0:
+                t_["f32", k] = work.tile([P, PACK, 512], F32, name="wide", tag="wide")
+            src = t_["bank", ("d", k), u][:].bitcast(BF16).rearrange("p (m e) -> p e m", e=2)
+            nc.scalar.activation(out=t_["f32", k][:, 2 * u : 2 * u + 2, :], in_=src, func=ACT.Ln)
+
+        def kernel_values(k, t):
+            if t == 0:
+                t_["u", k] = work.tile([P, PACK, 512], BF16, name="u_rows", tag="u_rows")
+            nc.vector.scalar_tensor_tensor(
+                out=t_["u", k][:, t, :],
+                in0=pair_half(("d", k), t),
+                scalar=t_["infl"][:, k % 4, t : t + 1],
+                in1=t_["f32", k][:, t, :],
+                op0=ALU.mult,
+                op1=ALU.mult,
+            )
+
+        def interleave(key, rows, lo, hi, on_scalar):
+            if ("grouped", key) not in t_:
+                t_["grouped", key] = grouped_tile("main", MAIN_BUFS)
+            if hi > lo:
+                engine_copy(
+                    on_scalar,
+                    t_["grouped", key][:, lo:hi, :].rearrange("p (c i) t -> p c t i", i=4),
+                    rows[:, :, lo:hi].rearrange("p t (c i) -> p c t i", i=4),
+                )
+
+        def group_a(h, lo, hi, on_scalar):
+            key = ("a", h)
+            if ("grouped", key) not in t_:
+                t_["grouped", key] = grouped_tile()
+            dst = t_["grouped", key][:].rearrange("p (t q e) j -> p q t j e", t=PACK, e=4)
+            src = t_["raw", key][:].rearrange("p j (q t e) -> p q t j e", t=PACK, e=4)
+            if hi > lo:
+                engine_copy(on_scalar, dst[:, lo:hi], src[:, lo:hi])
+
+        def group_v(h, g, lo, hi, on_scalar):
+            key = ("v", h, g)
+            if ("grouped", key) not in t_:
+                t_["grouped", key] = grouped_tile()
+            dst = t_["grouped", key][:].rearrange("p (t q) j -> p q j t", t=PACK)
+            src = t_["raw", ("v", h)][:, :, g * 512 : (g + 1) * 512].rearrange("p j (q t) -> p q j t", t=PACK)
+            if hi > lo:
+                engine_copy(on_scalar, dst[:, lo:hi], src[:, lo:hi])
+
+        def first_stage(b, h, t, i):
+            acc = bank(i)
+            cols = slice(t * P, (t + 1) * P)
+            a_codes, a_scales = t_["mx", ("a", h)]
+            x_codes, x_scales = t_["mx", ("x", b)]
+            nc.tensor.matmul_mx(
+                out=acc[:], lhsT=a_codes[:, cols].bitcast(FP8X4), lhsT_scale=a_scales[:, cols],
+                rhs=x_codes[:].bitcast(FP8X4), rhs_scale=x_scales[:], start=True, stop=False,
+            )
+            for g in range(4):
+                u_codes, u_scales = t_["mx", ("d", 4 * b + g)]
+                nc.tensor.matmul_mx(
+                    out=acc[:], lhsT=w_codes[:, g, h, t, :].bitcast(FP4X4), lhsT_scale=w_plane[:, g, h, t, :],
+                    rhs=u_codes[:].bitcast(FP8X4), rhs_scale=u_scales[:], start=False, stop=(g == 3),
+                )
+            t_["s", b, h, t] = acc
+
+        def bound(b, h, t):
+            if t == 0:
+                t_["tanh", b, h] = work.tile([P, PACK, 512], F32, name="wide", tag="wide")
+            nc.scalar.activation(out=t_["tanh", b, h][:, t, :], in_=t_["s", b, h, t][:], func=ACT.Tanh)
+
+        def latent(b, h):
+            t_["grouped", ("h", b, h)] = grouped_tile()
+            nc.vector.tensor_tensor(
+                out=t_["grouped", ("h", b, h)][:].rearrange("p (c i) t -> p c t i", i=4),
+                in0=t_["tanh", b, h][:].rearrange("p t (c i) -> p c t i", i=4),
+                in1=amp_cols[:, 4 * h : 4 * h + 4].unsqueeze(1).unsqueeze(3).broadcast_to([P, 128, PACK, 4]),
+                op=ALU.mult,
+            )
+
+        def base_term(b, g, t):
+            if t == 0:
+                t_["bb", b, g] = work.tile([P, PACK, 512], F32, name="base_term", tag="base_term")
+            nc.scalar.activation(
+                out=t_["bb", b, g][:, t, :], in_=pair_half(("b", b, g), t), func=ACT.Identity,
+                scale=spread_cols[:, g, t : t + 1], bias=shift_cols[:, g, t : t + 1],
+            )
+
+        def second_stage(b, g, t, i):
+            acc = bank(i)
+            cols = slice(t * P, (t + 1) * P)
+            for h in range(2):
+                v_codes, v_scales = t_["mx", ("v", h, g)]
+                h_codes, h_scales = t_["mx", ("h", b, h)]
+                nc.tensor.matmul_mx(
+                    out=acc[:], lhsT=v_codes[:, cols].bitcast(FP8X4), lhsT_scale=v_scales[:, cols],
+                    rhs=h_codes[:].bitcast(FP8X4), rhs_scale=h_scales[:], start=(h == 0), stop=(h == 1),
+                )
+            t_["acc", b, g, t] = acc
+
+        def finish(b, g, t):
+            if t == 0:
+                t_["y", b, g] = work.tile([P, PACK, 512], F32, name="y_rows", tag="y_rows")
+            nc.vector.scalar_tensor_tensor(
+                out=t_["y", b, g][:, t, :], in0=t_["acc", b, g, t][:], scalar=spread_cols[:, g, t : t + 1],
+                in1=t_["bb", b, g][:, t, :], op0=ALU.mult, op1=ALU.add,
+            )
+
+        def turn_back(b, g, r, i):
+            bk = bank(i)
+            for t in range(PACK):
+                nc.tensor.transpose(bk[:, t * P : (t + 1) * P], t_["y", b, g][:, t, r * P : (r + 1) * P], ident[:])
+            t_["back", b, g, r] = bk
+
+        def take_y(b, g, r, on_scalar=True):
+            rows = work.tile([P, P, PACK], F32, name="y_out", tag="y_out", bufs=6)
+            engine_copy(on_scalar, rows[:], t_["back", b, g, r][:].rearrange("m (t q) -> m q t", t=PACK))
+            m0 = b * MB + r * P
+            nc.sync.dma_start(out=out_0[m0 : m0 + P, g * 512 : (g + 1) * 512], in_=rows[:].rearrange("m q t -> m (q t)"))
+
+        def planes(b, g):
+            codes = work.tile([P, 512], U32, name="y_codes", tag="y_codes", align_bytes=64)
+            nc.vector.quantize_mx(
+                out=codes[:].bitcast(FP8X4),
+                scales=y_planes[b][:, g, :],
+                in_=t_["grouped", ("y", b, g)][:].rearrange("p m t -> p (m t)"),
+            )
+            dst = out_1[g, :, b * MB : (b + 1) * MB, :].rearrange("p m t -> p (m t)").bitcast(I32)
+            nc.sync.dma_start(out=dst, in_=codes[:].bitcast(I32))
+
+        def store_y_scales(b):
+            for q in range(4):
+                nc.sync.dma_start(
+                    out=out_2[:, 4 * q : 4 * q + 4, b * MB : (b + 1) * MB].rearrange("g r m -> r g m").bitcast(I32),
+                    in_=y_planes[b][32 * q : 32 * q + 4].bitcast(I32),
+                )
+
+        nc.vector.memset(warm[:], 1.0)
+        nc.scalar.activation(out=warm[:, 1:2], in_=warm[:, 0:1], func=ACT.Ln)
+        make_identity(nc, ident[:])
+        load_rows(("d", 0), d2, 0, 0)
+        load_columns("infl", influence, 4)
+        load_rows(("d", 1), d2, 0, 1)
+        load_rows(("d", 2), d2, 0, 2)
+        load_a(0)
+        load_rows(("d", 3), d2, 0, 3)
+        load_rows(("x", 0), x, 0, 0)
+        clear_w_scales()
+        nc.gpsimd.memset(amp_wide[:], 0.0)
+        load_w_scales()
+        load_w(0)
+        load_rows(("d", 4), d2, 1, 0)
+        load_w(1)
+        load_rows(("d", 5), d2, 1, 1)
+        load_a(1)
+        for u in range(2):
+            turn_pairs(("d", 0), u, u)
+        load_rows(("x", 1), x, 1, 0)
+        load_amp()
+        for k in range(8):
+            if k + 1 < 8:
+                for u in range(2):
+                    turn_pairs(("d", k + 1), u, 2 * ((k + 1) % 2) + u)
+            if k == 0:
+                load_rows(("d", 6), d2, 1, 2)
+            if k == 1:
+                load_rows(("d", 7), d2, 1, 3)
+                load_columns("spread_bf", spread, 3)
+                load_columns("bias_bf", bias, 3)
+                load_v(0)
+                load_v(1)
+            if k in (2, 3):
+                for half in range(2):
+                    turn_x(k - 2, half, 2 * k + half)
+            if k == 4:
+                amp_turn(4)
+            if k in (5, 6):
+                for t in range(2):
+                    first_stage(0, 0, 2 * (k - 5) + t, 4 + 2 * (k - 5) + t)
+            log_d2(k, 0)
+            log_d2(k, 1)
+            if k > 0:
+                interleave(("d", k - 1), t_["u", k - 1], U_SPLIT[k - 1], 512, False)
+                interleave(("d", k - 1), t_["u", k - 1], 0, U_SPLIT[k - 1], True)
+            if k == 6:
+                quantize(("a", 1), "a1")
+            for t in range(4):
+                kernel_values(k, t)
+            if k > 0:
+                quantize(("d", k - 1), "u%d" % (k - 1))
+            if k in (0, 1):
+                group_a(0, 16 * k, 16 * k + 16, True)
+            if k in (2, 3):
+                take_x(k - 2, 0)
+                take_x(k - 2, 1)
+            if k in (4, 5):
+                group_a(1, 16 * (k - 4), 16 * (k - 4) + 16, True)
+            if k == 2:
+                quantize(("a", 0), "a0")
+            if k in (3, 4):
+                quantize(("x", k - 3), "x%d" % (k - 3))
+            if k == 1:
+                deal_w_scales()
+            if k in (2, 4):
+                deal_w(k // 4)
+            if k == 3:
+                amp_widen()
+            if k == 4:
+                amp_take()
+            if k == 5:
+                channel_constants()
+            if 3 <= k:
+                load_rows(("b",) + UNITS[k - 3], base, *UNITS[k - 3])
+        load_rows(("b", 1, 2), base, 1, 2)
+        ring = [0, 1, 2, 3, 4, 5, 6, 7]
+        count = [0]
+
+        def nxt():
+            count[0] = count[0] + 1
+            return ring[(count[0] - 1) % 8]
+
+        def s_unit(b, h, ts):
+            for t in ts:
+                first_stage(b, h, t, nxt())
+
+        def tanh_unit(b, h, ts):
+            for t in ts:
+                bound(b, h, t)
+
+        def h_unit(b, h):
+            latent(b, h)
+
+        def hq(b, h):
+            quantize(("h", b, h), "h%d%d" % (b, h))
+
+        def vq(h, g):
+            quantize(("v", h, g), "v%d%d" % (h, g))
+
+        def base_unit(b, g):
+            for u in range(2):
+                turn_pairs(("b", b, g), u, nxt())
+            for t in range(4):
+                base_term(b, g, t)
+
+        def y_unit(b, g):
+            for t in range(4):
+                second_stage(b, g, t, nxt())
+                finish(b, g, t)
+
+        def back_unit(b, g):
+            for r in range(4):
+                turn_back(b, g, r, nxt())
+                take_y(b, g, r)
+
+        def cast(b, g):
+            interleave(("y", b, g), t_["y", b, g], 0, 512, False)
+
+        def y_half(b, g, half):
+            for t in (2 * half, 2 * half + 1):
+                second_stage(b, g, t, nxt())
+                finish(b, g, t)
+
+        def base_turn(b, g):
+            for u in range(2):
+                turn_pairs(("b", b, g), u, nxt())
+
+        def base_take(b, g):
+            for t in range(4):
+                base_term(b, g, t)
+
+        s_unit(0, 1, (0, 1))
+        tanh_unit(0, 0, range(4))
+        interleave(("d", 7), t_["u", 7], 0, 512, False)
+        s_unit(0, 1, (2, 3))
+        group_v(0, 0, 0, 128, False)
+        quantize(("d", 7), "u7")
+        h_unit(0, 0)
+        vq(0, 0)
+        tanh_unit(0, 1, range(4))
+        hq(0, 0)
+        base_unit(0, 0)
+        h_unit(0, 1)
+        group_v(1, 0, 0, 128, True)
+        s_unit(1, 0, range(4))
+        hq(0, 1)
+        vq(1, 0)
+        group_v(0, 1, 0, 128, False)
+        tanh_unit(1, 0, range(4))
+        vq(0, 1)
+        group_v(1, 1, 0, 128, False)
+        y_half(0, 0, 0)
+        vq(1, 1)
+        base_unit(0, 1)
+        y_half(0, 0, 1)
+        h_unit(1, 0)
+        s_unit(1, 1, (0, 1))
+        group_v(0, 2, 0, 128, True)
+        cast(0, 0)
+        hq(1, 0)
+        tanh_unit(1, 1, (0, 1))
+        y_half(0, 1, 0)
+        planes(0, 0)
+        back_unit(0, 0)
+        y_half(0, 1, 1)
+        vq(0, 2)
+        group_v(1, 2, 0, 128, False)
+        base_unit(0, 2)
+        s_unit(1, 1, (2, 3))
+        vq(1, 2)
+        cast(0, 1)
+        tanh_unit(1, 1, (2, 3))
+        planes(0, 1)
+        units = [(0, 1), (0, 2), (1, 0), (1, 1), (1, 2)]
+        for j in range(1, 5):
+            b, g = units[j]
+            y_half(b, g, 0)
+            if j == 1:
+                h_unit(1, 1)
+                hq(1, 1)
+            if j > 1:
+                planes(*units[j - 1])
+            if j == 2:
+                store_y_scales(0)
+            back_unit(*units[j - 1])
+            y_half(b, g, 1)
+            if j + 1 < len(units):
+                base_unit(*units[j + 1])
+            cast(b, g)
+        back_unit(1, 2)
+        planes(1, 2)
+        store_y_scales(1)

@@ -20,9 +20,11 @@ P = 128
 PACK = 4
 KP = 512
 MB = 512
-U_SPLIT = [256, 224, 224, 224, 224, 224, 0]
-MAIN_BUFS = 2
-UNITS = [(0, 0), (0, 1), (0, 2), (1, 0), (1, 1), (1, 2)]
+U_SPLIT = 0
+MAIN_BUFS = 1
+UNITS = [(0, 0), (0, 1), (1, 0), (1, 1), (0, 2), (1, 2)]
+RAW_SLOT = {"ws": 0, ("d", 0): 1, ("a", 0): 2, ("d", 1): 3, ("d", 2): 4, ("x", 0): 5, ("d", 3): 6, ("w", 0): 7, ("d", 4): 8, ("w", 1): 9, ("a", 1): 10, ("d", 5): 11, ("x", 1): 1, ("d", 6): 2, ("d", 7): 3, ("b",) + UNITS[0]: 4, ("b",) + UNITS[1]: 5, ("b",) + UNITS[2]: 6, ("b",) + UNITS[3]: 0, ("b",) + UNITS[4]: 8, ("b",) + UNITS[5]: 7}
+SPLIT = 160
 
 
 def tile_thin_plate_kernel_warp_k6_kernel(
@@ -40,15 +42,16 @@ def tile_thin_plate_kernel_warp_k6_kernel(
         def bank(i):
             return psum.tile([P, 512], F32, name="bank%d" % i, tag="bank%d" % i)
 
-        def raw_tile(shape, dtype):
-            return work.tile(shape, dtype, name="raw", tag="raw", bufs=12, align_bytes=64)
+        def raw_tile(key, shape, dtype):
+            tag = "raw%d" % RAW_SLOT[key]
+            return keep.tile(shape, dtype, name=tag, tag=tag, align_bytes=64)
 
         def codes_tiles(name):
             codes = keep.tile([P, 512], U32, name=name + "_codes", align_bytes=64)
             scales = keep.tile([P, 512], U8, name=name + "_scales", align_bytes=64)
             return codes, scales
 
-        def grouped_tile(tag="grouped", bufs=3):
+        def grouped_tile(tag="grouped", bufs=4):
             return work.tile([P, 512, PACK], BF16, name=tag, tag=tag, bufs=bufs, align_bytes=64)
 
         def quantize(key, name):
@@ -65,25 +68,25 @@ def tile_thin_plate_kernel_warp_k6_kernel(
                 nc.vector.tensor_copy(out=out, in_=in_)
 
         def load_rows(key, src, b, g):
-            raw = raw_tile([P, PACK, 512], BF16)
+            raw = raw_tile(key, [P, PACK, 512], BF16)
             view = src[b * MB : (b + 1) * MB, g * 512 : (g + 1) * 512].rearrange("(i p) c -> p i c", p=P)
             nc.sync.dma_start(out=raw[:], in_=view)
             t_["raw", key] = raw
 
         def load_a(h):
-            raw = raw_tile([P, PACK, 512], BF16)
+            raw = raw_tile(("a", h), [P, PACK, 512], BF16)
             nc.sync.dma_start(out=raw[:], in_=a[:, h * 512 : (h + 1) * 512].rearrange("(p j) f -> p j f", j=PACK))
             t_["raw", ("a", h)] = raw
 
         def load_w(pair):
-            raw = raw_tile([P, 2, 2048], U8)
+            raw = raw_tile(("w", pair), [P, 2, 2048], U8)
             nc.sync.dma_start(
                 out=raw[:].bitcast(I32), in_=w_words[2 * pair : 2 * pair + 2].rearrange("g p n -> p g n").bitcast(I32)
             )
             t_["raw", ("w", pair)] = raw
 
         def clear_w_scales():
-            raw = raw_tile([P, 4, 1024], U8)
+            raw = raw_tile("ws", [P, 4, 1024], U8)
             nc.gpsimd.memset(raw[:].bitcast(I32), 0)
             t_["raw", "ws"] = raw
 
@@ -123,9 +126,7 @@ def tile_thin_plate_kernel_warp_k6_kernel(
         shift_cols = keep.tile([P, 3, PACK], F32, name="shift_cols")
         w_codes = keep.tile([P, 4, 2, PACK, 256], U8, name="w_codes", align_bytes=64)
         w_plane = keep.tile([P, 4, 2, PACK, 128], U8, name="w_plane", align_bytes=64)
-        y_plane0 = keep.tile([P, 3, MB], U8, name="y_plane0", align_bytes=64)
-        y_plane1 = keep.tile([P, 3, MB], U8, name="y_plane1", align_bytes=64)
-        y_planes = [y_plane0, y_plane1]
+        y_plane = keep.tile([P, 3, M], U8, name="y_plane", align_bytes=64)
         warm = keep.tile([P, 2], F32, name="warm")
 
         def amp_widen():
@@ -171,13 +172,14 @@ def tile_thin_plate_kernel_warp_k6_kernel(
                     nc.tensor.transpose(bk[:, col : col + P], words[:, 2 * half + r, u:256:2], ident[:])
             t_["bank", ("x", b), half] = bk
 
-        def take_x(b, half):
+        def take_x(b, half, on_scalar=True):
             if half == 0:
                 t_["grouped", ("x", b)] = grouped_tile()
             words = t_["grouped", ("x", b)][:].rearrange("p m t -> p (m t)").bitcast(F32)
-            nc.scalar.copy(
-                out=words[:, half * 512 : (half + 1) * 512].rearrange("p (r m u) -> p r m u", r=2, u=2),
-                in_=t_["bank", ("x", b), half][:].rearrange("p (r u m) -> p r m u", r=2, u=2),
+            engine_copy(
+                on_scalar,
+                words[:, half * 512 : (half + 1) * 512].rearrange("p (r m u) -> p r m u", r=2, u=2),
+                t_["bank", ("x", b), half][:].rearrange("p (r u m) -> p r m u", r=2, u=2),
             )
 
         def log_d2(k, u):
@@ -207,6 +209,15 @@ def tile_thin_plate_kernel_warp_k6_kernel(
                     t_["grouped", key][:, lo:hi, :].rearrange("p (c i) t -> p c t i", i=4),
                     rows[:, :, lo:hi].rearrange("p t (c i) -> p c t i", i=4),
                 )
+
+        def interleave_pool(key, rows, lo, hi):
+            if ("grouped", key) not in t_:
+                t_["grouped", key] = grouped_tile("main", MAIN_BUFS)
+            nc.gpsimd.tensor_scalar(
+                out=t_["grouped", key][:, lo:hi, :],
+                in0=rows[:, :, lo:hi].rearrange("p t m -> p m t"),
+                scalar1=1.0, scalar2=0.0, op0=ALU.mult, op1=ALU.add,
+            )
 
         def group_a(h, lo, hi, on_scalar):
             key = ("a", h)
@@ -243,13 +254,31 @@ def tile_thin_plate_kernel_warp_k6_kernel(
                 )
             t_["s", b, h, t] = acc
 
+        def first_stage_pass(b, h, t, step, i=None):
+            if step == 0:
+                t_["s", b, h, t] = bank(i)
+                cols = slice(t * P, (t + 1) * P)
+                a_codes, a_scales = t_["mx", ("a", h)]
+                x_codes, x_scales = t_["mx", ("x", b)]
+                nc.tensor.matmul_mx(
+                    out=t_["s", b, h, t][:], lhsT=a_codes[:, cols].bitcast(FP8X4), lhsT_scale=a_scales[:, cols],
+                    rhs=x_codes[:].bitcast(FP8X4), rhs_scale=x_scales[:], start=True, stop=False,
+                )
+            else:
+                g = step - 1
+                u_codes, u_scales = t_["mx", ("d", 4 * b + g)]
+                nc.tensor.matmul_mx(
+                    out=t_["s", b, h, t][:], lhsT=w_codes[:, g, h, t, :].bitcast(FP4X4), lhsT_scale=w_plane[:, g, h, t, :],
+                    rhs=u_codes[:].bitcast(FP8X4), rhs_scale=u_scales[:], start=False, stop=(g == 3),
+                )
+
         def bound(b, h, t):
             if t == 0:
                 t_["tanh", b, h] = work.tile([P, PACK, 512], F32, name="wide", tag="wide")
             nc.scalar.activation(out=t_["tanh", b, h][:, t, :], in_=t_["s", b, h, t][:], func=ACT.Tanh)
 
-        def latent(b, h):
-            t_["grouped", ("h", b, h)] = grouped_tile()
+        def latent(b, h, main=False):
+            t_["grouped", ("h", b, h)] = grouped_tile("main", MAIN_BUFS) if main else grouped_tile()
             nc.vector.tensor_tensor(
                 out=t_["grouped", ("h", b, h)][:].rearrange("p (c i) t -> p c t i", i=4),
                 in0=t_["tanh", b, h][:].rearrange("p t (c i) -> p c t i", i=4),
@@ -285,6 +314,44 @@ def tile_thin_plate_kernel_warp_k6_kernel(
                 in1=t_["bb", b, g][:, t, :], op0=ALU.mult, op1=ALU.add,
             )
 
+        def second_stage_half(b, g, half, banks):
+            ms = slice(half * 256, (half + 1) * 256)
+            for pair in range(2):
+                acc = bank(banks[pair])
+                for e in range(2):
+                    t = 2 * pair + e
+                    cols = slice(t * P, (t + 1) * P)
+                    for h in range(2):
+                        v_codes, v_scales = t_["mx", ("v", h, g)]
+                        h_codes, h_scales = t_["mx", ("h", b, h)]
+                        nc.tensor.matmul_mx(
+                            out=acc[:, e * 256 : (e + 1) * 256], lhsT=v_codes[:, cols].bitcast(FP8X4), lhsT_scale=v_scales[:, cols],
+                            rhs=h_codes[:, ms].bitcast(FP8X4), rhs_scale=h_scales[:, ms], start=(h == 0), stop=(h == 1),
+                        )
+                t_["acc", half, pair] = acc
+
+        def finish_half(b, g, half):
+            if half == 0:
+                t_["y", b, g] = work.tile([P, PACK, 512], F32, name="y_rows", tag="y_rows")
+            ms = slice(half * 256, (half + 1) * 256)
+            for t in range(PACK):
+                nc.vector.scalar_tensor_tensor(
+                    out=t_["y", b, g][:, t, ms], in0=t_["acc", half, t // 2][:, (t % 2) * 256 : (t % 2 + 1) * 256],
+                    scalar=spread_cols[:, g, t : t + 1], in1=t_["bb", b, g][:, t, ms], op0=ALU.mult, op1=ALU.add,
+                )
+
+        def planes_half(b, g, half):
+            codes = work.tile([P, 512], U32, name="y_codes", tag="y_codes", bufs=3, align_bytes=64)
+            ms = slice(half * 256, (half + 1) * 256)
+            nc.vector.quantize_mx(
+                out=codes[:, 0:256].bitcast(FP8X4),
+                scales=y_plane[:, g, b * MB + half * 256 : b * MB + half * 256 + 256],
+                in_=t_["grouped", ("y", b, g)][:, ms, :].rearrange("p m t -> p (m t)"),
+            )
+            m0 = b * MB + half * 256
+            dst = out_1[g, :, m0 : m0 + 256, :].rearrange("p m t -> p (m t)").bitcast(I32)
+            nc.sync.dma_start(out=dst, in_=codes[:, 0:256].bitcast(I32))
+
         def turn_back(b, g, r, i):
             bk = bank(i)
             for t in range(PACK):
@@ -298,99 +365,22 @@ def tile_thin_plate_kernel_warp_k6_kernel(
             nc.sync.dma_start(out=out_0[m0 : m0 + P, g * 512 : (g + 1) * 512], in_=rows[:].rearrange("m q t -> m (q t)"))
 
         def planes(b, g):
-            codes = work.tile([P, 512], U32, name="y_codes", tag="y_codes", align_bytes=64)
+            codes = work.tile([P, 512], U32, name="y_codes", tag="y_codes", bufs=3, align_bytes=64)
             nc.vector.quantize_mx(
                 out=codes[:].bitcast(FP8X4),
-                scales=y_planes[b][:, g, :],
+                scales=y_plane[:, g, b * MB : (b + 1) * MB],
                 in_=t_["grouped", ("y", b, g)][:].rearrange("p m t -> p (m t)"),
             )
             dst = out_1[g, :, b * MB : (b + 1) * MB, :].rearrange("p m t -> p (m t)").bitcast(I32)
             nc.sync.dma_start(out=dst, in_=codes[:].bitcast(I32))
 
-        def store_y_scales(b):
+        def store_y_scales():
             for q in range(4):
                 nc.sync.dma_start(
-                    out=out_2[:, 4 * q : 4 * q + 4, b * MB : (b + 1) * MB].rearrange("g r m -> r g m").bitcast(I32),
-                    in_=y_planes[b][32 * q : 32 * q + 4].bitcast(I32),
+                    out=out_2[:, 4 * q : 4 * q + 4, :].rearrange("g r m -> r g m").bitcast(I32),
+                    in_=y_plane[32 * q : 32 * q + 4].bitcast(I32),
                 )
 
-        nc.vector.memset(warm[:], 1.0)
-        nc.scalar.activation(out=warm[:, 1:2], in_=warm[:, 0:1], func=ACT.Ln)
-        make_identity(nc, ident[:])
-        load_rows(("d", 0), d2, 0, 0)
-        load_columns("infl", influence, 4)
-        load_rows(("d", 1), d2, 0, 1)
-        load_rows(("d", 2), d2, 0, 2)
-        load_a(0)
-        load_rows(("d", 3), d2, 0, 3)
-        load_rows(("x", 0), x, 0, 0)
-        clear_w_scales()
-        nc.gpsimd.memset(amp_wide[:], 0.0)
-        load_w_scales()
-        load_w(0)
-        load_rows(("d", 4), d2, 1, 0)
-        load_w(1)
-        load_rows(("d", 5), d2, 1, 1)
-        load_a(1)
-        for u in range(2):
-            turn_pairs(("d", 0), u, u)
-        load_rows(("x", 1), x, 1, 0)
-        load_amp()
-        for k in range(8):
-            if k + 1 < 8:
-                for u in range(2):
-                    turn_pairs(("d", k + 1), u, 2 * ((k + 1) % 2) + u)
-            if k == 0:
-                load_rows(("d", 6), d2, 1, 2)
-            if k == 1:
-                load_rows(("d", 7), d2, 1, 3)
-                load_columns("spread_bf", spread, 3)
-                load_columns("bias_bf", bias, 3)
-                load_v(0)
-                load_v(1)
-            if k in (2, 3):
-                for half in range(2):
-                    turn_x(k - 2, half, 2 * k + half)
-            if k == 4:
-                amp_turn(4)
-            if k in (5, 6):
-                for t in range(2):
-                    first_stage(0, 0, 2 * (k - 5) + t, 4 + 2 * (k - 5) + t)
-            log_d2(k, 0)
-            log_d2(k, 1)
-            if k > 0:
-                interleave(("d", k - 1), t_["u", k - 1], U_SPLIT[k - 1], 512, False)
-                interleave(("d", k - 1), t_["u", k - 1], 0, U_SPLIT[k - 1], True)
-            if k == 6:
-                quantize(("a", 1), "a1")
-            for t in range(4):
-                kernel_values(k, t)
-            if k > 0:
-                quantize(("d", k - 1), "u%d" % (k - 1))
-            if k in (0, 1):
-                group_a(0, 16 * k, 16 * k + 16, True)
-            if k in (2, 3):
-                take_x(k - 2, 0)
-                take_x(k - 2, 1)
-            if k in (4, 5):
-                group_a(1, 16 * (k - 4), 16 * (k - 4) + 16, True)
-            if k == 2:
-                quantize(("a", 0), "a0")
-            if k in (3, 4):
-                quantize(("x", k - 3), "x%d" % (k - 3))
-            if k == 1:
-                deal_w_scales()
-            if k in (2, 4):
-                deal_w(k // 4)
-            if k == 3:
-                amp_widen()
-            if k == 4:
-                amp_take()
-            if k == 5:
-                channel_constants()
-            if 3 <= k:
-                load_rows(("b",) + UNITS[k - 3], base, *UNITS[k - 3])
-        load_rows(("b", 1, 2), base, 1, 2)
         ring = [0, 1, 2, 3, 4, 5, 6, 7]
         count = [0]
 
@@ -447,64 +437,183 @@ def tile_thin_plate_kernel_warp_k6_kernel(
             for t in range(4):
                 base_term(b, g, t)
 
-        s_unit(0, 1, (0, 1))
+        nc.vector.memset(warm[:], 1.0)
+        nc.scalar.activation(out=warm[:, 1:2], in_=warm[:, 0:1], func=ACT.Ln)
+        make_identity(nc, ident[:])
+        clear_w_scales()
+        nc.gpsimd.memset(amp_wide[:], 0.0)
+        load_rows(("d", 0), d2, 0, 0)
+        load_a(0)
+        load_columns("infl", influence, 4)
+        load_rows(("d", 1), d2, 0, 1)
+        load_rows(("d", 2), d2, 0, 2)
+        load_rows(("x", 0), x, 0, 0)
+        load_rows(("d", 3), d2, 0, 3)
+        load_w_scales()
+        load_amp()
+        for u in range(2):
+            turn_pairs(("d", 0), u, u)
+        group_a(0, 0, 32, False)
+        load_rows(("x", 1), x, 1, 0)
+        load_w(0)
+        load_rows(("d", 4), d2, 1, 0)
+        load_w(1)
+        load_rows(("d", 5), d2, 1, 1)
+        load_a(1)
+        load_rows(("d", 6), d2, 1, 2)
+        for k in range(8):
+            if k + 1 < 8:
+                for u in range(2):
+                    turn_pairs(("d", k + 1), u, 2 * ((k + 1) % 2) + u)
+            if k == 0:
+                load_rows(("d", 7), d2, 1, 3)
+                load_columns("spread_bf", spread, 3)
+                load_columns("bias_bf", bias, 3)
+                load_v(1)
+                load_v(0)
+            if k in (1, 2):
+                for half in range(2):
+                    turn_x(k - 1, half, 2 + 2 * k + half)
+            log_d2(k, 0)
+            log_d2(k, 1)
+            if k in (2, 3):
+                take_x(k - 2, 0)
+                take_x(k - 2, 1)
+            if k == 2:
+                quantize(("a", 0), "a0")
+                deal_w_scales()
+            if k == 3:
+                amp_widen()
+                amp_turn(4)
+                quantize(("x", 0), "x0")
+            if k in (3, 4):
+                deal_w(k - 3)
+            if k == 5:
+                group_a(1, 16, 32, False)
+            if k == 6:
+                quantize(("a", 1), "a1")
+            if k == 7:
+                channel_constants()
+                quantize(("x", 1), "x1")
+            if k > 1:
+                quantize(("d", k - 2), "u%d" % (k - 2))
+            if k == 4:
+                for step in range(3):
+                    for t in range(4):
+                        first_stage_pass(0, 0, t, step, 4 + t)
+            if k == 5:
+                for step in range(3, 5):
+                    for t in range(4):
+                        first_stage_pass(0, 0, t, step)
+            if k == 7:
+                s_unit(0, 1, (0, 1))
+            if k > 0:
+                interleave_pool(("d", k - 1), t_["u", k - 1], SPLIT, 512)
+            if 0 < k < 7:
+                interleave(("d", k - 1), t_["u", k - 1], 0, SPLIT, True)
+            for t in range(4):
+                kernel_values(k, t)
+            if k == 7:
+                interleave(("d", k - 1), t_["u", k - 1], 0, SPLIT, False)
+            if k == 3:
+                amp_take()
+            if k == 4:
+                group_a(1, 0, 16, True)
+            if 2 <= k:
+                load_rows(("b",) + UNITS[k - 2], base, *UNITS[k - 2])
+        def y_mm(j, half):
+            b, g = UNITS[j]
+            for t in (2 * half, 2 * half + 1):
+                second_stage(b, g, t, nxt())
+
+        def y_fin(j):
+            for t in range(4):
+                finish(*UNITS[j], t)
+
+        def cast_j(j, lo, hi, how):
+            b, g = UNITS[j]
+            if how == "pool":
+                interleave_pool(("y", b, g), t_["y", b, g], lo, hi)
+            else:
+                interleave(("y", b, g), t_["y", b, g], lo, hi, how == "act")
+
         tanh_unit(0, 0, range(4))
+        quantize(("d", 6), "u6")
         interleave(("d", 7), t_["u", 7], 0, 512, False)
         s_unit(0, 1, (2, 3))
-        group_v(0, 0, 0, 128, False)
-        quantize(("d", 7), "u7")
+        for step in range(4):
+            for t in range(4):
+                first_stage_pass(1, 0, t, step, nxt() if step == 0 else None)
         h_unit(0, 0)
-        vq(0, 0)
+        quantize(("d", 7), "u7")
+        for t in range(4):
+            first_stage_pass(1, 0, t, 4)
         tanh_unit(0, 1, range(4))
+        group_v(1, 0, 0, 128, False)
         hq(0, 0)
-        base_unit(0, 0)
-        h_unit(0, 1)
-        group_v(1, 0, 0, 128, True)
-        s_unit(1, 0, range(4))
-        hq(0, 1)
-        vq(1, 0)
-        group_v(0, 1, 0, 128, False)
+        group_v(0, 0, 0, 128, True)
+        base_turn(*UNITS[0])
         tanh_unit(1, 0, range(4))
-        vq(0, 1)
-        group_v(1, 1, 0, 128, False)
-        y_half(0, 0, 0)
-        vq(1, 1)
-        base_unit(0, 1)
-        y_half(0, 0, 1)
+        base_take(*UNITS[0])
+        h_unit(0, 1)
+        vq(1, 0)
+        hq(0, 1)
+        vq(0, 0)
+        s_unit(1, 1, range(4))
         h_unit(1, 0)
-        s_unit(1, 1, (0, 1))
-        group_v(0, 2, 0, 128, True)
-        cast(0, 0)
+        group_v(0, 1, 0, 128, True)
+        group_v(1, 1, 0, 128, False)
         hq(1, 0)
-        tanh_unit(1, 1, (0, 1))
-        y_half(0, 1, 0)
-        planes(0, 0)
-        back_unit(0, 0)
-        y_half(0, 1, 1)
-        vq(0, 2)
-        group_v(1, 2, 0, 128, False)
-        base_unit(0, 2)
-        s_unit(1, 1, (2, 3))
-        vq(1, 2)
-        cast(0, 1)
-        tanh_unit(1, 1, (2, 3))
-        planes(0, 1)
-        units = [(0, 1), (0, 2), (1, 0), (1, 1), (1, 2)]
-        for j in range(1, 5):
-            b, g = units[j]
-            y_half(b, g, 0)
+        vq(1, 1)
+        tanh_unit(1, 1, range(4))
+        vq(0, 1)
+        for j in range(5):
+            y_mm(j, 0)
+            if j > 0:
+                for r in range(4):
+                    turn_back(*UNITS[j - 1], r, nxt())
+            y_mm(j, 1)
             if j == 1:
-                h_unit(1, 1)
+                latent(1, 1, True)
                 hq(1, 1)
-            if j > 1:
-                planes(*units[j - 1])
+            if 1 < j:
+                cast_j(j - 2, 0, SPLIT, "dve")
             if j == 2:
-                store_y_scales(0)
-            back_unit(*units[j - 1])
-            y_half(b, g, 1)
-            if j + 1 < len(units):
-                base_unit(*units[j + 1])
-            cast(b, g)
-        back_unit(1, 2)
-        planes(1, 2)
-        store_y_scales(1)
+                group_v(0, 2, 0, 128, False)
+            if j == 3:
+                vq(0, 2)
+                vq(1, 2)
+            if j > 1:
+                planes(*UNITS[j - 2])
+            if 0 < j:
+                cast_j(j - 1, SPLIT, 512, "pool")
+            for t in range(4):
+                finish(*UNITS[j], t)
+            if j == 2:
+                group_v(1, 2, 0, 128, False)
+            if 0 < j:
+                for r in range(4):
+                    take_y(*UNITS[j - 1], r)
+            base_unit(*UNITS[j + 1])
+        last = UNITS[5]
+        second_stage_half(*last, 0, (nxt(), nxt()))
+        for r in range(4):
+            turn_back(*UNITS[4], r, nxt())
+        second_stage_half(*last, 1, (nxt(), nxt()))
+        cast_j(3, 0, SPLIT, "dve")
+        planes(*UNITS[3])
+        cast_j(4, 0, 512, "dve")
+        finish_half(*last, 0)
+        for r in range(4):
+            take_y(*UNITS[4], r)
+        planes(*UNITS[4])
+        finish_half(*last, 1)
+        for r in range(4):
+            turn_back(*last, r, nxt())
+        take_y(*last, 0)
+        take_y(*last, 1)
+        cast_j(5, 0, 512, "dve")
+        take_y(*last, 2)
+        take_y(*last, 3)
+        planes(*last)
+        store_y_scales()

@@ -13,607 +13,548 @@ I32 = mybir.dt.int32
 U8 = mybir.dt.uint8
 FP8X4 = mybir.dt.float8_e4m3fn_x4
 FP4X4 = mybir.dt.float4_e2m1fn_x4
-ACT = mybir.ActivationFunctionType
+FUNC = mybir.ActivationFunctionType
 ALU = mybir.AluOpType
 
 P = 128
-PACK = 4
-KP = 512
-MB = 512
-U_SPLIT = 0
-MAIN_BUFS = 1
-UNITS = [(0, 0), (0, 1), (1, 0), (1, 1), (0, 2), (1, 2)]
-RAW_SLOT = {"ws": 0, ("d", 0): 1, ("a", 0): 2, ("d", 1): 3, ("d", 2): 4, ("x", 0): 5, ("d", 3): 6, ("w", 0): 7, ("d", 4): 8, ("w", 1): 9, ("a", 1): 10, ("d", 5): 11, ("x", 1): 1, ("d", 6): 2, ("d", 7): 3, ("b",) + UNITS[0]: 4, ("b",) + UNITS[1]: 5, ("b",) + UNITS[2]: 6, ("b",) + UNITS[3]: 0, ("b",) + UNITS[4]: 8, ("b",) + UNITS[5]: 7}
-SPLIT = 160
+SLOTS = 4
+GROUP = P * SLOTS
+POINTS = 512
+TILES = POINTS // P
+HALF = POINTS // 2
+BANKS = 8
+U_GROUPS, LATENT_GROUPS, CHANNEL_GROUPS = C // GROUP, F // GROUP, N // GROUP
+U_PIECES = (M // POINTS) * U_GROUPS
+Y_PIECES = [(0, 0), (0, 1), (1, 0), (1, 1), (0, 2), (1, 2)]
+U_REST = 160
+Y_REST = 192
+LANDING = [
+    ["w_scales", ("base", 3)],
+    [("d2", 0, 0), ("x", 1)],
+    [("a", 0), ("d2", 6)],
+    [("d2", 1), ("d2", 7)],
+    [("d2", 2), ("base", 0)],
+    [("x", 0), ("base", 1)],
+    [("d2", 3), ("base", 2)],
+    [("w", 0), ("base", 5)],
+    [("d2", 4), ("base", 4)],
+    [("w", 1)],
+    [("a", 1)],
+    [("d2", 0, 1), ("d2", 5)],
+]
 
 
 def tile_thin_plate_kernel_warp_k6_kernel(
     tc, d2, influence, w_words, w_scales, x, a, amp, v, bias, base, spread, out_0, out_1, out_2
 ):
     nc = tc.nc
+    scalar_copy, vector_copy = nc.scalar.copy, nc.vector.tensor_copy
     with ExitStack() as ctx:
         keep = ctx.enter_context(tc.tile_pool(name="keep", bufs=1))
         work = ctx.enter_context(tc.tile_pool(name="work", bufs=2))
         psum = ctx.enter_context(tc.psum_pool(name="psum", bufs=1))
         ctx.enter_context(tc.manual_schedule())
 
-        t_ = {}
+        loaded, banks, rows, packed, mx = {}, {}, {}, {}, {}
+        place = {key: i for i, keys in enumerate(LANDING) for key in keys}
+        handed_out = []
 
         def bank(i):
-            return psum.tile([P, 512], F32, name="bank%d" % i, tag="bank%d" % i)
+            return psum.tile([P, POINTS], F32, name="bank%d" % i, tag="bank%d" % i)
 
-        def raw_tile(key, shape, dtype):
-            tag = "raw%d" % RAW_SLOT[key]
-            return keep.tile(shape, dtype, name=tag, tag=tag, align_bytes=64)
+        def next_bank():
+            handed_out.append(len(handed_out) % BANKS)
+            return bank(handed_out[-1])
 
-        def codes_tiles(name):
-            codes = keep.tile([P, 512], U32, name=name + "_codes", align_bytes=64)
-            scales = keep.tile([P, 512], U8, name=name + "_scales", align_bytes=64)
-            return codes, scales
+        def landing_tile(key, shape, dtype):
+            tag = "landing%d" % place[key]
+            loaded[key] = keep.tile(shape, dtype, name=tag, tag=tag, align_bytes=64)
+            return loaded[key]
 
-        def grouped_tile(tag="grouped", bufs=4):
-            return work.tile([P, 512, PACK], BF16, name=tag, tag=tag, bufs=bufs, align_bytes=64)
+        def packed_tile(key, shared):
+            if key not in packed:
+                tag, bufs = ("shared", 1) if shared else ("packed", 4)
+                packed[key] = work.tile([P, POINTS, SLOTS], BF16, name=tag, tag=tag, bufs=bufs, align_bytes=64)
+            return packed[key]
 
-        def quantize(key, name):
-            codes, scales = codes_tiles(name)
+        def quantize(*key):
+            name = "_".join(str(part) for part in key)
+            codes = keep.tile([P, POINTS], U32, name=name + "_codes", align_bytes=64)
+            scales = keep.tile([P, POINTS], U8, name=name + "_scales", align_bytes=64)
             nc.vector.quantize_mx(
-                out=codes[:].bitcast(FP8X4), scales=scales[:], in_=t_["grouped", key][:].rearrange("p m t -> p (m t)")
+                out=codes[:].bitcast(FP8X4), scales=scales[:], in_=packed[key][:].rearrange("p m t -> p (m t)")
             )
-            t_["mx", key] = (codes, scales)
+            mx[key] = (codes, scales)
 
-        def engine_copy(on_scalar, out, in_):
-            if on_scalar:
-                nc.scalar.copy(out=out, in_=in_)
-            else:
-                nc.vector.tensor_copy(out=out, in_=in_)
+        def mx_pass(out, weight, weight_scales, moving, points, start, stop):
+            codes, scales = mx[moving]
+            nc.tensor.matmul_mx(
+                out=out,
+                lhsT=weight,
+                lhsT_scale=weight_scales,
+                rhs=codes[:, points].bitcast(FP8X4),
+                rhs_scale=scales[:, points],
+                start=start,
+                stop=stop,
+            )
 
-        def load_rows(key, src, b, g):
-            raw = raw_tile(key, [P, PACK, 512], BF16)
-            view = src[b * MB : (b + 1) * MB, g * 512 : (g + 1) * 512].rearrange("(i p) c -> p i c", p=P)
-            nc.sync.dma_start(out=raw[:], in_=view)
-            t_["raw", key] = raw
+        ident = keep.tile([P, P], F32, name="ident")
+        amp_square = keep.tile([P, P], F32, name="amp_square")
+        amp_cols = keep.tile([P, LATENT_GROUPS * SLOTS], F32, name="amp_cols")
+        spread_cols = keep.tile([P, CHANNEL_GROUPS, SLOTS], F32, name="spread_cols")
+        shift_cols = keep.tile([P, CHANNEL_GROUPS, SLOTS], F32, name="shift_cols")
+        w_codes = keep.tile([P, U_GROUPS, LATENT_GROUPS, SLOTS, 2 * P], U8, name="w_codes", align_bytes=64)
+        w_plane = keep.tile([P, U_GROUPS, LATENT_GROUPS, SLOTS, P], U8, name="w_plane", align_bytes=64)
+        y_plane = keep.tile([P, CHANNEL_GROUPS, M], U8, name="y_plane", align_bytes=64)
+        warm = keep.tile([P, 2], F32, name="warm")
+
+        def load_points(key, src, first_point, tiles, group):
+            view = src[first_point : first_point + tiles * P, group * GROUP : (group + 1) * GROUP]
+            tile = landing_tile(key, [P, tiles, GROUP], BF16)
+            nc.sync.dma_start(out=tile[:], in_=view.rearrange("(i p) c -> p i c", p=P))
+
+        def load_d2(k):
+            load_points(("d2", k), d2, k // U_GROUPS * POINTS, TILES, k % U_GROUPS)
+
+        def load_base(j):
+            b, g = Y_PIECES[j]
+            load_points(("base", j), base, b * POINTS, TILES, g)
 
         def load_a(h):
-            raw = raw_tile(("a", h), [P, PACK, 512], BF16)
-            nc.sync.dma_start(out=raw[:], in_=a[:, h * 512 : (h + 1) * 512].rearrange("(p j) f -> p j f", j=PACK))
-            t_["raw", ("a", h)] = raw
+            tile = landing_tile(("a", h), [P, SLOTS, GROUP], BF16)
+            view = a[:, h * GROUP : (h + 1) * GROUP].rearrange("(p t) f -> p t f", t=SLOTS)
+            nc.sync.dma_start(out=tile[:], in_=view)
 
         def load_w(pair):
-            raw = raw_tile(("w", pair), [P, 2, 2048], U8)
-            nc.sync.dma_start(
-                out=raw[:].bitcast(I32), in_=w_words[2 * pair : 2 * pair + 2].rearrange("g p n -> p g n").bitcast(I32)
-            )
-            t_["raw", ("w", pair)] = raw
-
-        def clear_w_scales():
-            raw = raw_tile("ws", [P, 4, 1024], U8)
-            nc.gpsimd.memset(raw[:].bitcast(I32), 0)
-            t_["raw", "ws"] = raw
+            tile = landing_tile(("w", pair), [P, 2, 2 * F], U8)
+            view = w_words[2 * pair : 2 * pair + 2].rearrange("g p n -> p g n")
+            nc.sync.dma_start(out=tile[:].bitcast(I32), in_=view.bitcast(I32))
 
         def load_w_scales():
-            raw = t_["raw", "ws"]
             for q in range(4):
                 nc.sync.dma_start(
-                    out=raw[32 * q : 32 * q + 4].bitcast(I32),
+                    out=loaded["w_scales"][32 * q : 32 * q + 4].bitcast(I32),
                     in_=w_scales[:, 4 * q : 4 * q + 4, :].rearrange("g r n -> r g n").bitcast(I32),
                 )
 
         def load_v(h):
-            raw = keep.tile([P, PACK, N], BF16, name="v_raw%d" % h)
-            rows = v[h * 512 : (h + 1) * 512, :].rearrange("(q t e) n -> e q t n", t=PACK, e=4)
+            loaded["v", h] = keep.tile([P, SLOTS, N], BF16, name="v_rows%d" % h)
+            view = v[h * GROUP : (h + 1) * GROUP, :].rearrange("(r t e) n -> e r t n", t=SLOTS, e=4)
             for e in range(4):
-                nc.sync.dma_start(out=raw[e:P:4], in_=rows[e])
-            t_["raw", ("v", h)] = raw
+                nc.sync.dma_start(out=loaded["v", h][e:P:4], in_=view[e])
 
         def load_columns(name, vec, groups):
-            cols = keep.tile([P, groups, PACK], BF16, name=name)
-            nc.sync.dma_start(out=cols[:], in_=vec.rearrange("(g p t) -> p g t", p=P, t=PACK))
-            t_[name] = cols
+            loaded[name] = keep.tile([P, groups, SLOTS], BF16, name=name)
+            nc.sync.dma_start(out=loaded[name][:], in_=vec.rearrange("(g p t) -> p g t", p=P, t=SLOTS))
 
         def load_amp():
-            rows = keep.tile([8, P], BF16, name="amp_rows")
-            for h in range(2):
+            loaded["amp"] = keep.tile([LATENT_GROUPS * SLOTS, P], BF16, name="amp_rows")
+            for h in range(LATENT_GROUPS):
                 nc.sync.dma_start(
-                    out=rows[4 * h : 4 * h + 4].rearrange("t (q e) -> t q e", e=4),
-                    in_=amp[h * 512 : (h + 1) * 512].rearrange("(q t e) -> t q e", t=PACK, e=4),
+                    out=loaded["amp"][SLOTS * h : SLOTS * (h + 1)].rearrange("t (r e) -> t r e", e=4),
+                    in_=amp[h * GROUP : (h + 1) * GROUP].rearrange("(r t e) -> t r e", t=SLOTS, e=4),
                 )
-            t_["amp_rows"] = rows
-
-        ident = keep.tile([P, P], F32, name="ident")
-        amp_wide = keep.tile([P, P], F32, name="amp_wide")
-        amp_cols = keep.tile([P, 8], F32, name="amp_cols")
-        spread_cols = keep.tile([P, 3, PACK], F32, name="spread_cols")
-        shift_cols = keep.tile([P, 3, PACK], F32, name="shift_cols")
-        w_codes = keep.tile([P, 4, 2, PACK, 256], U8, name="w_codes", align_bytes=64)
-        w_plane = keep.tile([P, 4, 2, PACK, 128], U8, name="w_plane", align_bytes=64)
-        y_plane = keep.tile([P, 3, M], U8, name="y_plane", align_bytes=64)
-        warm = keep.tile([P, 2], F32, name="warm")
-
-        def amp_widen():
-            nc.vector.tensor_copy(out=amp_wide[0:8], in_=t_["amp_rows"][:])
-
-        def amp_turn(i):
-            t_["amp_bank"] = bank(i)
-            nc.tensor.transpose(t_["amp_bank"][:, 0:P], amp_wide[:], ident[:])
-
-        def amp_take():
-            nc.vector.tensor_copy(out=amp_cols[:], in_=t_["amp_bank"][:, 0:8])
-
-        def channel_constants():
-            nc.vector.tensor_copy(out=spread_cols[:], in_=t_["spread_bf"][:])
-            nc.vector.tensor_tensor(out=shift_cols[:], in0=t_["bias_bf"][:], in1=t_["spread_bf"][:], op=ALU.mult)
 
         def deal_w(pair):
-            src = t_["raw", ("w", pair)][:].bitcast(I32).rearrange("p g (h q t w) -> p (g h) t q w", h=2, t=PACK, w=2)
-            dst = w_codes[:, 2 * pair : 2 * pair + 2].bitcast(I32).rearrange("p g h t (q w) -> p (g h) t q w", w=2)
-            nc.vector.tensor_copy(out=dst, in_=src)
+            src = loaded["w", pair][:].bitcast(I32).rearrange("p g (h r t w) -> p (g h) t r w", h=2, t=SLOTS, w=2)
+            dst = w_codes[:, 2 * pair : 2 * pair + 2].bitcast(I32).rearrange("p g h t (r w) -> p (g h) t r w", w=2)
+            vector_copy(out=dst, in_=src)
 
         def deal_w_scales():
-            src = t_["raw", "ws"][:].bitcast(I32).rearrange("p g (h q t) -> p (g h) q t", h=2, t=PACK)
-            dst = w_plane[:].bitcast(I32).rearrange("p g h t q -> p (g h) q t")
-            nc.vector.tensor_copy(out=dst, in_=src)
+            src = loaded["w_scales"][:].bitcast(I32).rearrange("p g (h r t) -> p (g h) r t", h=2, t=SLOTS)
+            vector_copy(out=w_plane[:].bitcast(I32).rearrange("p g h t r -> p (g h) r t"), in_=src)
 
-        def turn_pairs(key, u, i):
-            words = t_["raw", key][:].bitcast(F32)
-            bk = bank(i)
-            for r in range(4):
-                nc.tensor.transpose(bk[:, r * P : (r + 1) * P], words[:, r, u:256:2], ident[:])
-            t_["bank", key, u] = bk
+        def pack_a(h, runs, copy):
+            dst = packed_tile(("a", h), False)[:].rearrange("p (t r e) s -> p r t s e", t=SLOTS, e=4)
+            src = loaded["a", h][:].rearrange("p s (r t e) -> p r t s e", t=SLOTS, e=4)
+            copy(out=dst[:, runs], in_=src[:, runs])
 
-        def pair_half(key, t):
-            return t_["bank", key, t // 2][:].bitcast(BF16)[:, t % 2 : 1024 : 2]
+        def pack_v(h, g, columns, copy):
+            dst = packed_tile(("v", h, g), False)[:].rearrange("p (t q) s -> p q s t", t=SLOTS)
+            src = loaded["v", h][:, :, g * GROUP : (g + 1) * GROUP].rearrange("p s (q t) -> p q s t", t=SLOTS)
+            copy(out=dst[:, columns], in_=src[:, columns])
 
-        def turn_x(b, half, i):
-            words = t_["raw", ("x", b)][:].bitcast(F32)
-            bk = bank(i)
-            for r in range(2):
+        def turn_amp(i):
+            vector_copy(out=amp_square[0 : LATENT_GROUPS * SLOTS], in_=loaded["amp"][:])
+            banks["amp"] = bank(i)
+            nc.tensor.transpose(banks["amp"][:, 0:P], amp_square[:], ident[:])
+
+        def channel_constants():
+            vector_copy(out=spread_cols[:], in_=loaded["spread"][:])
+            nc.vector.tensor_tensor(out=shift_cols[:], in0=loaded["bias"][:], in1=loaded["spread"][:], op=ALU.mult)
+
+        def turn_words(dst, key, i, u):
+            nc.tensor.transpose(dst, loaded[key][:].bitcast(F32)[:, i, u : GROUP // 2 : 2], ident[:])
+
+        def turn_pairs(key, u, into):
+            banks[key, u] = into
+            for i in range(TILES):
+                turn_words(into[:, i * P : (i + 1) * P], key, i, u)
+
+        def slot_of(key, t):
+            return banks[key, t // 2][:].bitcast(BF16)[:, t % 2 : 2 * POINTS : 2]
+
+        def turn_x(b, half, into):
+            banks[("x", b), half] = into
+            for i in range(2):
                 for u in range(2):
-                    col = (2 * r + u) * P
-                    nc.tensor.transpose(bk[:, col : col + P], words[:, 2 * half + r, u:256:2], ident[:])
-            t_["bank", ("x", b), half] = bk
+                    turn_words(into[:, (2 * i + u) * P : (2 * i + u + 1) * P], ("x", b), 2 * half + i, u)
 
-        def take_x(b, half, on_scalar=True):
-            if half == 0:
-                t_["grouped", ("x", b)] = grouped_tile()
-            words = t_["grouped", ("x", b)][:].rearrange("p m t -> p (m t)").bitcast(F32)
-            engine_copy(
-                on_scalar,
-                words[:, half * 512 : (half + 1) * 512].rearrange("p (r m u) -> p r m u", r=2, u=2),
-                t_["bank", ("x", b), half][:].rearrange("p (r u m) -> p r m u", r=2, u=2),
-            )
-
-        def log_d2(k, u):
-            if u == 0:
-                t_["f32", k] = work.tile([P, PACK, 512], F32, name="wide", tag="wide")
-            src = t_["bank", ("d", k), u][:].bitcast(BF16).rearrange("p (m e) -> p e m", e=2)
-            nc.scalar.activation(out=t_["f32", k][:, 2 * u : 2 * u + 2, :], in_=src, func=ACT.Ln)
-
-        def kernel_values(k, t):
-            if t == 0:
-                t_["u", k] = work.tile([P, PACK, 512], BF16, name="u_rows", tag="u_rows")
-            nc.vector.scalar_tensor_tensor(
-                out=t_["u", k][:, t, :],
-                in0=pair_half(("d", k), t),
-                scalar=t_["infl"][:, k % 4, t : t + 1],
-                in1=t_["f32", k][:, t, :],
-                op0=ALU.mult,
-                op1=ALU.mult,
-            )
-
-        def interleave(key, rows, lo, hi, on_scalar):
-            if ("grouped", key) not in t_:
-                t_["grouped", key] = grouped_tile("main", MAIN_BUFS)
-            if hi > lo:
-                engine_copy(
-                    on_scalar,
-                    t_["grouped", key][:, lo:hi, :].rearrange("p (c i) t -> p c t i", i=4),
-                    rows[:, :, lo:hi].rearrange("p t (c i) -> p c t i", i=4),
+        def pack_x(b):
+            words = packed_tile(("x", b), False)[:].rearrange("p m t -> p (m t)").bitcast(F32)
+            for half in range(2):
+                scalar_copy(
+                    out=words[:, half * POINTS : (half + 1) * POINTS].rearrange("p (i m u) -> p i m u", i=2, u=2),
+                    in_=banks[("x", b), half][:].rearrange("p (i u m) -> p i m u", i=2, u=2),
                 )
 
-        def interleave_pool(key, rows, lo, hi):
-            if ("grouped", key) not in t_:
-                t_["grouped", key] = grouped_tile("main", MAIN_BUFS)
+        def pack(key, points, copy, shared=True):
+            copy(
+                out=packed_tile(key, shared)[:, points, :].rearrange("p (c i) t -> p c t i", i=4),
+                in_=rows[key][:, :, points].rearrange("p t (c i) -> p c t i", i=4),
+            )
+
+        def pack_on_gpsimd(key, points):
             nc.gpsimd.tensor_scalar(
-                out=t_["grouped", key][:, lo:hi, :],
-                in0=rows[:, :, lo:hi].rearrange("p t m -> p m t"),
-                scalar1=1.0, scalar2=0.0, op0=ALU.mult, op1=ALU.add,
+                out=packed_tile(key, True)[:, points, :],
+                in0=rows[key][:, :, points].rearrange("p t m -> p m t"),
+                scalar1=1.0,
+                scalar2=0.0,
+                op0=ALU.mult,
+                op1=ALU.add,
             )
 
-        def group_a(h, lo, hi, on_scalar):
-            key = ("a", h)
-            if ("grouped", key) not in t_:
-                t_["grouped", key] = grouped_tile()
-            dst = t_["grouped", key][:].rearrange("p (t q e) j -> p q t j e", t=PACK, e=4)
-            src = t_["raw", key][:].rearrange("p j (q t e) -> p q t j e", t=PACK, e=4)
-            if hi > lo:
-                engine_copy(on_scalar, dst[:, lo:hi], src[:, lo:hi])
+        def log_d2(k):
+            rows["log", k] = work.tile([P, SLOTS, POINTS], F32, name="scalar_rows", tag="scalar_rows")
+            for u in range(2):
+                src = banks[("d2", k), u][:].bitcast(BF16).rearrange("p (m e) -> p e m", e=2)
+                nc.scalar.activation(out=rows["log", k][:, 2 * u : 2 * u + 2, :], in_=src, func=FUNC.Ln)
 
-        def group_v(h, g, lo, hi, on_scalar):
-            key = ("v", h, g)
-            if ("grouped", key) not in t_:
-                t_["grouped", key] = grouped_tile()
-            dst = t_["grouped", key][:].rearrange("p (t q) j -> p q j t", t=PACK)
-            src = t_["raw", ("v", h)][:, :, g * 512 : (g + 1) * 512].rearrange("p j (q t) -> p q j t", t=PACK)
-            if hi > lo:
-                engine_copy(on_scalar, dst[:, lo:hi], src[:, lo:hi])
-
-        def first_stage(b, h, t, i):
-            acc = bank(i)
-            cols = slice(t * P, (t + 1) * P)
-            a_codes, a_scales = t_["mx", ("a", h)]
-            x_codes, x_scales = t_["mx", ("x", b)]
-            nc.tensor.matmul_mx(
-                out=acc[:], lhsT=a_codes[:, cols].bitcast(FP8X4), lhsT_scale=a_scales[:, cols],
-                rhs=x_codes[:].bitcast(FP8X4), rhs_scale=x_scales[:], start=True, stop=False,
-            )
-            for g in range(4):
-                u_codes, u_scales = t_["mx", ("d", 4 * b + g)]
-                nc.tensor.matmul_mx(
-                    out=acc[:], lhsT=w_codes[:, g, h, t, :].bitcast(FP4X4), lhsT_scale=w_plane[:, g, h, t, :],
-                    rhs=u_codes[:].bitcast(FP8X4), rhs_scale=u_scales[:], start=False, stop=(g == 3),
+        def u_values(k):
+            rows["u", k] = work.tile([P, SLOTS, POINTS], BF16, name="u_rows", tag="u_rows")
+            for t in range(SLOTS):
+                nc.vector.scalar_tensor_tensor(
+                    out=rows["u", k][:, t, :],
+                    in0=slot_of(("d2", k), t),
+                    scalar=loaded["influence"][:, k % U_GROUPS, t : t + 1],
+                    in1=rows["log", k][:, t, :],
+                    op0=ALU.mult,
+                    op1=ALU.mult,
                 )
-            t_["s", b, h, t] = acc
 
-        def first_stage_pass(b, h, t, step, i=None):
+        def s_pass(b, h, t, step):
             if step == 0:
-                t_["s", b, h, t] = bank(i)
-                cols = slice(t * P, (t + 1) * P)
-                a_codes, a_scales = t_["mx", ("a", h)]
-                x_codes, x_scales = t_["mx", ("x", b)]
-                nc.tensor.matmul_mx(
-                    out=t_["s", b, h, t][:], lhsT=a_codes[:, cols].bitcast(FP8X4), lhsT_scale=a_scales[:, cols],
-                    rhs=x_codes[:].bitcast(FP8X4), rhs_scale=x_scales[:], start=True, stop=False,
-                )
+                codes, scales = mx["a", h]
+                columns = slice(t * P, (t + 1) * P)
+                weight, weight_scales, moving = codes[:, columns].bitcast(FP8X4), scales[:, columns], ("x", b)
             else:
                 g = step - 1
-                u_codes, u_scales = t_["mx", ("d", 4 * b + g)]
-                nc.tensor.matmul_mx(
-                    out=t_["s", b, h, t][:], lhsT=w_codes[:, g, h, t, :].bitcast(FP4X4), lhsT_scale=w_plane[:, g, h, t, :],
-                    rhs=u_codes[:].bitcast(FP8X4), rhs_scale=u_scales[:], start=False, stop=(g == 3),
-                )
+                weight, weight_scales = w_codes[:, g, h, t, :].bitcast(FP4X4), w_plane[:, g, h, t, :]
+                moving = ("u", U_GROUPS * b + g)
+            mx_pass(banks["s", b, h, t][:], weight, weight_scales, moving, slice(None), step == 0, step == U_GROUPS)
 
-        def bound(b, h, t):
-            if t == 0:
-                t_["tanh", b, h] = work.tile([P, PACK, 512], F32, name="wide", tag="wide")
-            nc.scalar.activation(out=t_["tanh", b, h][:, t, :], in_=t_["s", b, h, t][:], func=ACT.Tanh)
+        def s_by_bank(b, h, slots):
+            for t in slots:
+                banks["s", b, h, t] = next_bank()
+                for step in range(U_GROUPS + 1):
+                    s_pass(b, h, t, step)
 
-        def latent(b, h, main=False):
-            t_["grouped", ("h", b, h)] = grouped_tile("main", MAIN_BUFS) if main else grouped_tile()
+        def s_by_pass(b, h, steps):
+            for step in steps:
+                for t in range(SLOTS):
+                    s_pass(b, h, t, step)
+
+        def tanh_s(b, h):
+            rows["tanh", b, h] = work.tile([P, SLOTS, POINTS], F32, name="scalar_rows", tag="scalar_rows")
+            for t in range(SLOTS):
+                nc.scalar.activation(out=rows["tanh", b, h][:, t, :], in_=banks["s", b, h, t][:], func=FUNC.Tanh)
+
+        def h_values(b, h, shared=False):
+            gains = amp_cols[:, SLOTS * h : SLOTS * (h + 1)].unsqueeze(1).unsqueeze(3)
             nc.vector.tensor_tensor(
-                out=t_["grouped", ("h", b, h)][:].rearrange("p (c i) t -> p c t i", i=4),
-                in0=t_["tanh", b, h][:].rearrange("p t (c i) -> p c t i", i=4),
-                in1=amp_cols[:, 4 * h : 4 * h + 4].unsqueeze(1).unsqueeze(3).broadcast_to([P, 128, PACK, 4]),
+                out=packed_tile(("h", b, h), shared)[:].rearrange("p (c i) t -> p c t i", i=4),
+                in0=rows["tanh", b, h][:].rearrange("p t (c i) -> p c t i", i=4),
+                in1=gains.broadcast_to([P, POINTS // 4, SLOTS, 4]),
                 op=ALU.mult,
             )
 
-        def base_term(b, g, t):
-            if t == 0:
-                t_["bb", b, g] = work.tile([P, PACK, 512], F32, name="base_term", tag="base_term")
-            nc.scalar.activation(
-                out=t_["bb", b, g][:, t, :], in_=pair_half(("b", b, g), t), func=ACT.Identity,
-                scale=spread_cols[:, g, t : t + 1], bias=shift_cols[:, g, t : t + 1],
-            )
-
-        def second_stage(b, g, t, i):
-            acc = bank(i)
-            cols = slice(t * P, (t + 1) * P)
-            for h in range(2):
-                v_codes, v_scales = t_["mx", ("v", h, g)]
-                h_codes, h_scales = t_["mx", ("h", b, h)]
-                nc.tensor.matmul_mx(
-                    out=acc[:], lhsT=v_codes[:, cols].bitcast(FP8X4), lhsT_scale=v_scales[:, cols],
-                    rhs=h_codes[:].bitcast(FP8X4), rhs_scale=h_scales[:], start=(h == 0), stop=(h == 1),
+        def base_term(j, slots):
+            g = Y_PIECES[j][1]
+            if ("base", j) not in rows:
+                rows["base", j] = work.tile([P, SLOTS, POINTS], F32, name="base_rows", tag="base_rows")
+            for t in slots:
+                nc.scalar.activation(
+                    out=rows["base", j][:, t, :],
+                    in_=slot_of(("base", j), t),
+                    func=FUNC.Identity,
+                    scale=spread_cols[:, g, t : t + 1],
+                    bias=shift_cols[:, g, t : t + 1],
                 )
-            t_["acc", b, g, t] = acc
 
-        def finish(b, g, t):
-            if t == 0:
-                t_["y", b, g] = work.tile([P, PACK, 512], F32, name="y_rows", tag="y_rows")
-            nc.vector.scalar_tensor_tensor(
-                out=t_["y", b, g][:, t, :], in0=t_["acc", b, g, t][:], scalar=spread_cols[:, g, t : t + 1],
-                in1=t_["bb", b, g][:, t, :], op0=ALU.mult, op1=ALU.add,
-            )
+        def y_product(j, t, points, out):
+            b, g = Y_PIECES[j]
+            banks["y", j, t, points.start] = out
+            columns = slice(t * P, (t + 1) * P)
+            for h in range(LATENT_GROUPS):
+                codes, scales = mx["v", h, g]
+                weight = codes[:, columns].bitcast(FP8X4)
+                mx_pass(out, weight, scales[:, columns], ("h", b, h), points, h == 0, h == LATENT_GROUPS - 1)
 
-        def second_stage_half(b, g, half, banks):
-            ms = slice(half * 256, (half + 1) * 256)
-            for pair in range(2):
-                acc = bank(banks[pair])
-                for e in range(2):
-                    t = 2 * pair + e
-                    cols = slice(t * P, (t + 1) * P)
-                    for h in range(2):
-                        v_codes, v_scales = t_["mx", ("v", h, g)]
-                        h_codes, h_scales = t_["mx", ("h", b, h)]
-                        nc.tensor.matmul_mx(
-                            out=acc[:, e * 256 : (e + 1) * 256], lhsT=v_codes[:, cols].bitcast(FP8X4), lhsT_scale=v_scales[:, cols],
-                            rhs=h_codes[:, ms].bitcast(FP8X4), rhs_scale=h_scales[:, ms], start=(h == 0), stop=(h == 1),
-                        )
-                t_["acc", half, pair] = acc
-
-        def finish_half(b, g, half):
-            if half == 0:
-                t_["y", b, g] = work.tile([P, PACK, 512], F32, name="y_rows", tag="y_rows")
-            ms = slice(half * 256, (half + 1) * 256)
-            for t in range(PACK):
+        def y_values(j, slots, points):
+            g = Y_PIECES[j][1]
+            if ("y", j) not in rows:
+                rows["y", j] = work.tile([P, SLOTS, POINTS], F32, name="y_rows", tag="y_rows")
+            for t in slots:
                 nc.vector.scalar_tensor_tensor(
-                    out=t_["y", b, g][:, t, ms], in0=t_["acc", half, t // 2][:, (t % 2) * 256 : (t % 2 + 1) * 256],
-                    scalar=spread_cols[:, g, t : t + 1], in1=t_["bb", b, g][:, t, ms], op0=ALU.mult, op1=ALU.add,
+                    out=rows["y", j][:, t, points],
+                    in0=banks["y", j, t, points.start],
+                    scalar=spread_cols[:, g, t : t + 1],
+                    in1=rows["base", j][:, t, points],
+                    op0=ALU.mult,
+                    op1=ALU.add,
                 )
 
-        def planes_half(b, g, half):
-            codes = work.tile([P, 512], U32, name="y_codes", tag="y_codes", bufs=3, align_bytes=64)
-            ms = slice(half * 256, (half + 1) * 256)
+        def turn_y(j, tiles):
+            for i in tiles:
+                banks["turned", j, i] = next_bank()
+                for t in range(SLOTS):
+                    nc.tensor.transpose(
+                        banks["turned", j, i][:, t * P : (t + 1) * P], rows["y", j][:, t, i * P : (i + 1) * P], ident[:]
+                    )
+
+        def store_y(j, tiles):
+            b, g = Y_PIECES[j]
+            for i in tiles:
+                out_tile = work.tile([P, P, SLOTS], F32, name="y_out", tag="y_out", bufs=6)
+                scalar_copy(out=out_tile[:], in_=banks["turned", j, i][:].rearrange("m (t q) -> m q t", t=SLOTS))
+                first = b * POINTS + i * P
+                nc.sync.dma_start(
+                    out=out_0[first : first + P, g * GROUP : (g + 1) * GROUP],
+                    in_=out_tile[:].rearrange("m q t -> m (q t)"),
+                )
+
+        def quantize_y(j):
+            b, g = Y_PIECES[j]
+            mx["y", j] = work.tile([P, POINTS], U32, name="y_codes", tag="y_codes", bufs=3, align_bytes=64)
             nc.vector.quantize_mx(
-                out=codes[:, 0:256].bitcast(FP8X4),
-                scales=y_plane[:, g, b * MB + half * 256 : b * MB + half * 256 + 256],
-                in_=t_["grouped", ("y", b, g)][:, ms, :].rearrange("p m t -> p (m t)"),
+                out=mx["y", j][:].bitcast(FP8X4),
+                scales=y_plane[:, g, b * POINTS : (b + 1) * POINTS],
+                in_=packed["y", j][:].rearrange("p m t -> p (m t)"),
             )
-            m0 = b * MB + half * 256
-            dst = out_1[g, :, m0 : m0 + 256, :].rearrange("p m t -> p (m t)").bitcast(I32)
-            nc.sync.dma_start(out=dst, in_=codes[:, 0:256].bitcast(I32))
 
-        def turn_back(b, g, r, i):
-            bk = bank(i)
-            for t in range(PACK):
-                nc.tensor.transpose(bk[:, t * P : (t + 1) * P], t_["y", b, g][:, t, r * P : (r + 1) * P], ident[:])
-            t_["back", b, g, r] = bk
+        def store_codes(j):
+            b, g = Y_PIECES[j]
+            dst = out_1[g, :, b * POINTS : (b + 1) * POINTS, :].rearrange("p m t -> p (m t)")
+            nc.sync.dma_start(out=dst.bitcast(I32), in_=mx["y", j][:].bitcast(I32))
 
-        def take_y(b, g, r, on_scalar=True):
-            rows = work.tile([P, P, PACK], F32, name="y_out", tag="y_out", bufs=6)
-            engine_copy(on_scalar, rows[:], t_["back", b, g, r][:].rearrange("m (t q) -> m q t", t=PACK))
-            m0 = b * MB + r * P
-            nc.sync.dma_start(out=out_0[m0 : m0 + P, g * 512 : (g + 1) * 512], in_=rows[:].rearrange("m q t -> m (q t)"))
-
-        def planes(b, g):
-            codes = work.tile([P, 512], U32, name="y_codes", tag="y_codes", bufs=3, align_bytes=64)
-            nc.vector.quantize_mx(
-                out=codes[:].bitcast(FP8X4),
-                scales=y_plane[:, g, b * MB : (b + 1) * MB],
-                in_=t_["grouped", ("y", b, g)][:].rearrange("p m t -> p (m t)"),
-            )
-            dst = out_1[g, :, b * MB : (b + 1) * MB, :].rearrange("p m t -> p (m t)").bitcast(I32)
-            nc.sync.dma_start(out=dst, in_=codes[:].bitcast(I32))
-
-        def store_y_scales():
+        def store_scales():
             for q in range(4):
                 nc.sync.dma_start(
                     out=out_2[:, 4 * q : 4 * q + 4, :].rearrange("g r m -> r g m").bitcast(I32),
                     in_=y_plane[32 * q : 32 * q + 4].bitcast(I32),
                 )
 
-        ring = [0, 1, 2, 3, 4, 5, 6, 7]
-        count = [0]
-
-        def nxt():
-            count[0] = count[0] + 1
-            return ring[(count[0] - 1) % 8]
-
-        def s_unit(b, h, ts):
-            for t in ts:
-                first_stage(b, h, t, nxt())
-
-        def tanh_unit(b, h, ts):
-            for t in ts:
-                bound(b, h, t)
-
-        def h_unit(b, h):
-            latent(b, h)
-
-        def hq(b, h):
-            quantize(("h", b, h), "h%d%d" % (b, h))
-
-        def vq(h, g):
-            quantize(("v", h, g), "v%d%d" % (h, g))
-
-        def base_unit(b, g):
-            for u in range(2):
-                turn_pairs(("b", b, g), u, nxt())
-            for t in range(4):
-                base_term(b, g, t)
-
-        def y_unit(b, g):
-            for t in range(4):
-                second_stage(b, g, t, nxt())
-                finish(b, g, t)
-
-        def back_unit(b, g):
-            for r in range(4):
-                turn_back(b, g, r, nxt())
-                take_y(b, g, r)
-
-        def cast(b, g):
-            interleave(("y", b, g), t_["y", b, g], 0, 512, False)
-
-        def y_half(b, g, half):
-            for t in (2 * half, 2 * half + 1):
-                second_stage(b, g, t, nxt())
-                finish(b, g, t)
-
-        def base_turn(b, g):
-            for u in range(2):
-                turn_pairs(("b", b, g), u, nxt())
-
-        def base_take(b, g):
-            for t in range(4):
-                base_term(b, g, t)
+        everything = slice(0, POINTS)
+        all_columns = slice(0, P)
 
         nc.vector.memset(warm[:], 1.0)
-        nc.scalar.activation(out=warm[:, 1:2], in_=warm[:, 0:1], func=ACT.Ln)
+        nc.scalar.activation(out=warm[:, 1:2], in_=warm[:, 0:1], func=FUNC.Ln)
         make_identity(nc, ident[:])
-        clear_w_scales()
-        nc.gpsimd.memset(amp_wide[:], 0.0)
-        load_rows(("d", 0), d2, 0, 0)
+        nc.gpsimd.memset(landing_tile("w_scales", [P, U_GROUPS, F], U8)[:].bitcast(I32), 0)
+        nc.gpsimd.memset(amp_square[:], 0.0)
+        for half in range(2):
+            load_points(("d2", 0, half), d2, half * HALF, 2, 0)
         load_a(0)
-        load_columns("infl", influence, 4)
-        load_rows(("d", 1), d2, 0, 1)
-        load_rows(("d", 2), d2, 0, 2)
-        load_rows(("x", 0), x, 0, 0)
-        load_rows(("d", 3), d2, 0, 3)
+        load_columns("influence", influence, U_GROUPS)
+        load_d2(1)
+        load_d2(2)
+        load_points(("x", 0), x, 0, TILES, 0)
+        load_d2(3)
         load_w_scales()
         load_amp()
         for u in range(2):
-            turn_pairs(("d", 0), u, u)
-        group_a(0, 0, 32, False)
-        load_rows(("x", 1), x, 1, 0)
+            banks[("d2", 0), u] = bank(u)
+        for half in range(2):
+            for u in range(2):
+                for i in range(2):
+                    column = (2 * half + i) * P
+                    turn_words(banks[("d2", 0), u][:, column : column + P], ("d2", 0, half), i, u)
+        pack_a(0, slice(0, 32), vector_copy)
+        load_points(("x", 1), x, POINTS, TILES, 0)
         load_w(0)
-        load_rows(("d", 4), d2, 1, 0)
+        load_d2(4)
         load_w(1)
-        load_rows(("d", 5), d2, 1, 1)
+        load_d2(5)
         load_a(1)
-        load_rows(("d", 6), d2, 1, 2)
-        for k in range(8):
-            if k + 1 < 8:
+        load_d2(6)
+
+        def round_0():
+            load_d2(7)
+            load_columns("spread", spread, CHANNEL_GROUPS)
+            load_columns("bias", bias, CHANNEL_GROUPS)
+            load_v(1)
+            load_v(0)
+
+        def round_2():
+            pack_x(0)
+            quantize("a", 0)
+            deal_w_scales()
+
+        def round_3():
+            pack_x(1)
+            turn_amp(4)
+            quantize("x", 0)
+            deal_w(0)
+
+        def round_7():
+            channel_constants()
+            quantize("x", 1)
+
+        on_the_side = {
+            0: round_0,
+            2: round_2,
+            3: round_3,
+            4: lambda: deal_w(1),
+            5: lambda: pack_a(1, slice(16, 32), vector_copy),
+            6: lambda: quantize("a", 1),
+            7: round_7,
+        }
+        last_u = U_PIECES - 1
+        for k in range(U_PIECES):
+            if k < last_u:
                 for u in range(2):
-                    turn_pairs(("d", k + 1), u, 2 * ((k + 1) % 2) + u)
-            if k == 0:
-                load_rows(("d", 7), d2, 1, 3)
-                load_columns("spread_bf", spread, 3)
-                load_columns("bias_bf", bias, 3)
-                load_v(1)
-                load_v(0)
+                    turn_pairs(("d2", k + 1), u, bank(2 * ((k + 1) % 2) + u))
             if k in (1, 2):
                 for half in range(2):
-                    turn_x(k - 1, half, 2 + 2 * k + half)
-            log_d2(k, 0)
-            log_d2(k, 1)
-            if k in (2, 3):
-                take_x(k - 2, 0)
-                take_x(k - 2, 1)
-            if k == 2:
-                quantize(("a", 0), "a0")
-                deal_w_scales()
-            if k == 3:
-                amp_widen()
-                amp_turn(4)
-                quantize(("x", 0), "x0")
-            if k in (3, 4):
-                deal_w(k - 3)
-            if k == 5:
-                group_a(1, 16, 32, False)
-            if k == 6:
-                quantize(("a", 1), "a1")
-            if k == 7:
-                channel_constants()
-                quantize(("x", 1), "x1")
+                    turn_x(k - 1, half, bank(2 + 2 * k + half))
+            log_d2(k)
+            if k in on_the_side:
+                on_the_side[k]()
             if k > 1:
-                quantize(("d", k - 2), "u%d" % (k - 2))
+                quantize("u", k - 2)
             if k == 4:
-                for step in range(3):
-                    for t in range(4):
-                        first_stage_pass(0, 0, t, step, 4 + t)
+                for t in range(SLOTS):
+                    banks["s", 0, 0, t] = bank(4 + t)
+                s_by_pass(0, 0, range(3))
             if k == 5:
-                for step in range(3, 5):
-                    for t in range(4):
-                        first_stage_pass(0, 0, t, step)
-            if k == 7:
-                s_unit(0, 1, (0, 1))
+                s_by_pass(0, 0, range(3, 5))
+            if k == last_u:
+                s_by_bank(0, 1, range(2))
             if k > 0:
-                interleave_pool(("d", k - 1), t_["u", k - 1], SPLIT, 512)
-            if 0 < k < 7:
-                interleave(("d", k - 1), t_["u", k - 1], 0, SPLIT, True)
-            for t in range(4):
-                kernel_values(k, t)
-            if k == 7:
-                interleave(("d", k - 1), t_["u", k - 1], 0, SPLIT, False)
+                pack_on_gpsimd(("u", k - 1), slice(U_REST, POINTS))
+            if 0 < k < last_u:
+                pack(("u", k - 1), slice(0, U_REST), scalar_copy)
+            u_values(k)
+            if k == last_u:
+                pack(("u", k - 1), slice(0, U_REST), vector_copy)
             if k == 3:
-                amp_take()
+                vector_copy(out=amp_cols[:], in_=banks["amp"][:, 0 : LATENT_GROUPS * SLOTS])
             if k == 4:
-                group_a(1, 0, 16, True)
-            if 2 <= k:
-                load_rows(("b",) + UNITS[k - 2], base, *UNITS[k - 2])
-        def y_mm(j, half):
-            b, g = UNITS[j]
+                pack_a(1, slice(0, 16), scalar_copy)
+            if k >= 2:
+                load_base(k - 2)
+
+        tanh_s(0, 0)
+        quantize("u", last_u - 1)
+        pack(("u", last_u), everything, vector_copy)
+        s_by_bank(0, 1, range(2, 4))
+        for t in range(SLOTS):
+            banks["s", 1, 0, t] = next_bank()
+        s_by_pass(1, 0, range(U_GROUPS))
+        h_values(0, 0)
+        quantize("u", last_u)
+        s_by_pass(1, 0, range(U_GROUPS, U_GROUPS + 1))
+        tanh_s(0, 1)
+        pack_v(1, 0, all_columns, vector_copy)
+        quantize("h", 0, 0)
+        pack_v(0, 0, all_columns, scalar_copy)
+        for u in range(2):
+            turn_pairs(("base", 0), u, next_bank())
+        tanh_s(1, 0)
+        base_term(0, range(SLOTS))
+        h_values(0, 1)
+        quantize("v", 1, 0)
+        quantize("h", 0, 1)
+        quantize("v", 0, 0)
+        s_by_bank(1, 1, range(SLOTS))
+        h_values(1, 0)
+        pack_v(0, 1, all_columns, scalar_copy)
+        pack_v(1, 1, all_columns, vector_copy)
+        quantize("h", 1, 0)
+        quantize("v", 1, 1)
+        tanh_s(1, 1)
+        quantize("v", 0, 1)
+
+        def product_half(j, half):
             for t in (2 * half, 2 * half + 1):
-                second_stage(b, g, t, nxt())
+                y_product(j, t, everything, next_bank()[:])
 
-        def y_fin(j):
-            for t in range(4):
-                finish(*UNITS[j], t)
-
-        def cast_j(j, lo, hi, how):
-            b, g = UNITS[j]
-            if how == "pool":
-                interleave_pool(("y", b, g), t_["y", b, g], lo, hi)
-            else:
-                interleave(("y", b, g), t_["y", b, g], lo, hi, how == "act")
-
-        tanh_unit(0, 0, range(4))
-        quantize(("d", 6), "u6")
-        interleave(("d", 7), t_["u", 7], 0, 512, False)
-        s_unit(0, 1, (2, 3))
-        for step in range(4):
-            for t in range(4):
-                first_stage_pass(1, 0, t, step, nxt() if step == 0 else None)
-        h_unit(0, 0)
-        quantize(("d", 7), "u7")
-        for t in range(4):
-            first_stage_pass(1, 0, t, 4)
-        tanh_unit(0, 1, range(4))
-        group_v(1, 0, 0, 128, False)
-        hq(0, 0)
-        group_v(0, 0, 0, 128, True)
-        base_turn(*UNITS[0])
-        tanh_unit(1, 0, range(4))
-        base_take(*UNITS[0])
-        h_unit(0, 1)
-        vq(1, 0)
-        hq(0, 1)
-        vq(0, 0)
-        s_unit(1, 1, range(4))
-        h_unit(1, 0)
-        group_v(0, 1, 0, 128, True)
-        group_v(1, 1, 0, 128, False)
-        hq(1, 0)
-        vq(1, 1)
-        tanh_unit(1, 1, range(4))
-        vq(0, 1)
-        for j in range(5):
-            y_mm(j, 0)
+        def turn_half(j, half):
             if j > 0:
-                for r in range(4):
-                    turn_back(*UNITS[j - 1], r, nxt())
-            y_mm(j, 1)
+                turn_y(j - 1, (2 * half, 2 * half + 1))
+            turn_pairs(("base", j + 1), half, next_bank())
+
+        def take_half(j, half):
+            if j > 0:
+                store_y(j - 1, (2 * half, 2 * half + 1))
+            base_term(j + 1, (2 * half, 2 * half + 1))
+
+        last_y = len(Y_PIECES) - 1
+        for j in range(last_y):
+            product_half(j, 0)
+            turn_half(j, 0)
+            product_half(j, 1)
             if j == 1:
-                latent(1, 1, True)
-                hq(1, 1)
-            if 1 < j:
-                cast_j(j - 2, 0, SPLIT, "dve")
-            if j == 2:
-                group_v(0, 2, 0, 128, False)
-            if j == 3:
-                vq(0, 2)
-                vq(1, 2)
+                h_values(1, 1, shared=True)
+                quantize("h", 1, 1)
             if j > 1:
-                planes(*UNITS[j - 2])
-            if 0 < j:
-                cast_j(j - 1, SPLIT, 512, "pool")
-            for t in range(4):
-                finish(*UNITS[j], t)
+                pack(("y", j - 2), slice(0, Y_REST), vector_copy)
             if j == 2:
-                group_v(1, 2, 0, 128, False)
-            if 0 < j:
-                for r in range(4):
-                    take_y(*UNITS[j - 1], r)
-            base_unit(*UNITS[j + 1])
-        last = UNITS[5]
-        second_stage_half(*last, 0, (nxt(), nxt()))
-        for r in range(4):
-            turn_back(*UNITS[4], r, nxt())
-        second_stage_half(*last, 1, (nxt(), nxt()))
-        cast_j(3, 0, SPLIT, "dve")
-        planes(*UNITS[3])
-        cast_j(4, 0, 512, "dve")
-        finish_half(*last, 0)
-        for r in range(4):
-            take_y(*UNITS[4], r)
-        planes(*UNITS[4])
-        finish_half(*last, 1)
-        for r in range(4):
-            turn_back(*last, r, nxt())
-        take_y(*last, 0)
-        take_y(*last, 1)
-        cast_j(5, 0, 512, "dve")
-        take_y(*last, 2)
-        take_y(*last, 3)
-        planes(*last)
-        store_y_scales()
+                pack_v(1, 2, all_columns, vector_copy)
+            if j == 3:
+                quantize("v", 0, 2)
+                quantize("v", 1, 2)
+            if j > 1:
+                quantize_y(j - 2)
+                store_codes(j - 2)
+            if 0 < j < last_y - 1:
+                pack_on_gpsimd(("y", j - 1), slice(Y_REST, POINTS))
+            if j == last_y - 1:
+                pack(("y", j - 1), everything, vector_copy)
+            y_values(j, range(2), everything)
+            if j == last_y - 1:
+                quantize_y(j - 1)
+            y_values(j, range(2, 4), everything)
+            take_half(j, 0)
+            if j == last_y - 1:
+                store_codes(j - 1)
+            turn_half(j, 1)
+            take_half(j, 1)
+            if j < 2:
+                pack_v(0, 2, slice(j * P // 2, (j + 1) * P // 2), scalar_copy)
+
+        halves = [slice(0, HALF), slice(HALF, POINTS)]
+
+        def last_product(points):
+            for pair in range(2):
+                both = next_bank()
+                for e in range(2):
+                    y_product(last_y, 2 * pair + e, points, both[:, e * HALF : (e + 1) * HALF])
+
+        last_product(halves[0])
+        turn_y(last_y - 1, range(TILES))
+        last_product(halves[1])
+        pack(("y", last_y - 1), everything, vector_copy)
+        y_values(last_y, range(SLOTS), halves[0])
+        quantize_y(last_y - 1)
+        store_y(last_y - 1, range(2))
+        store_codes(last_y - 1)
+        store_y(last_y - 1, range(2, TILES))
+        y_values(last_y, range(SLOTS), halves[1])
+        turn_y(last_y, range(TILES))
+        pack(("y", last_y), everything, vector_copy)
+        quantize_y(last_y)
+        store_y(last_y, range(3))
+        store_codes(last_y)
+        store_y(last_y, range(3, TILES))
+        store_scales()

from contextlib import ExitStack

import concourse.mybir as mybir
from concourse.masks import make_identity

M, C, D, F, N = 1024, 2048, 512, 1024, 1536
FLOPS = 2 * M * C * F + 2 * M * D * F + 2 * M * F * N

F32 = mybir.dt.float32
BF16 = mybir.dt.bfloat16
U32 = mybir.dt.uint32
I32 = mybir.dt.int32
U8 = mybir.dt.uint8
FP8X4 = mybir.dt.float8_e4m3fn_x4
FP4X4 = mybir.dt.float4_e2m1fn_x4
FUNC = mybir.ActivationFunctionType
ALU = mybir.AluOpType

P = 128
SLOTS = 4
GROUP = P * SLOTS
POINTS = 512
TILES = POINTS // P
HALF = POINTS // 2
BANKS = 8
U_GROUPS, LATENT_GROUPS, CHANNEL_GROUPS = C // GROUP, F // GROUP, N // GROUP
U_PIECES = (M // POINTS) * U_GROUPS
Y_PIECES = [(0, 0), (0, 1), (1, 0), (1, 1), (0, 2), (1, 2)]
U_REST = 160
Y_REST = 192
LANDING = [
    ["w_scales", ("base", 3)],
    [("d2", 0, 0), ("x", 1)],
    [("a", 0), ("d2", 6)],
    [("d2", 1), ("d2", 7)],
    [("d2", 2), ("base", 0)],
    [("x", 0), ("base", 1)],
    [("d2", 3), ("base", 2)],
    [("w", 0), ("base", 5)],
    [("d2", 4), ("base", 4)],
    [("w", 1)],
    [("a", 1)],
    [("d2", 0, 1), ("d2", 5)],
]


def tile_thin_plate_kernel_warp_k6_kernel(
    tc, d2, influence, w_words, w_scales, x, a, amp, v, bias, base, spread, out_0, out_1, out_2
):
    nc = tc.nc
    scalar_copy, vector_copy = nc.scalar.copy, nc.vector.tensor_copy
    with ExitStack() as ctx:
        keep = ctx.enter_context(tc.tile_pool(name="keep", bufs=1))
        work = ctx.enter_context(tc.tile_pool(name="work", bufs=2))
        psum = ctx.enter_context(tc.psum_pool(name="psum", bufs=1))
        ctx.enter_context(tc.manual_schedule())

        loaded, banks, rows, packed, mx = {}, {}, {}, {}, {}
        place = {key: i for i, keys in enumerate(LANDING) for key in keys}
        handed_out = []

        def bank(i):
            return psum.tile([P, POINTS], F32, name="bank%d" % i, tag="bank%d" % i)

        def next_bank():
            handed_out.append(len(handed_out) % BANKS)
            return bank(handed_out[-1])

        def landing_tile(key, shape, dtype):
            tag = "landing%d" % place[key]
            loaded[key] = keep.tile(shape, dtype, name=tag, tag=tag, align_bytes=64)
            return loaded[key]

        def packed_tile(key, shared):
            if key not in packed:
                tag, bufs = ("shared", 1) if shared else ("packed", 4)
                packed[key] = work.tile([P, POINTS, SLOTS], BF16, name=tag, tag=tag, bufs=bufs, align_bytes=64)
            return packed[key]

        def quantize(*key):
            name = "_".join(str(part) for part in key)
            codes = keep.tile([P, POINTS], U32, name=name + "_codes", align_bytes=64)
            scales = keep.tile([P, POINTS], U8, name=name + "_scales", align_bytes=64)
            nc.vector.quantize_mx(
                out=codes[:].bitcast(FP8X4), scales=scales[:], in_=packed[key][:].rearrange("p m t -> p (m t)")
            )
            mx[key] = (codes, scales)

        def mx_pass(out, weight, weight_scales, moving, points, start, stop):
            codes, scales = mx[moving]
            nc.tensor.matmul_mx(
                out=out,
                lhsT=weight,
                lhsT_scale=weight_scales,
                rhs=codes[:, points].bitcast(FP8X4),
                rhs_scale=scales[:, points],
                start=start,
                stop=stop,
            )

        ident = keep.tile([P, P], F32, name="ident")
        amp_square = keep.tile([P, P], F32, name="amp_square")
        amp_cols = keep.tile([P, LATENT_GROUPS * SLOTS], F32, name="amp_cols")
        spread_cols = keep.tile([P, CHANNEL_GROUPS, SLOTS], F32, name="spread_cols")
        shift_cols = keep.tile([P, CHANNEL_GROUPS, SLOTS], F32, name="shift_cols")
        w_codes = keep.tile([P, U_GROUPS, LATENT_GROUPS, SLOTS, 2 * P], U8, name="w_codes", align_bytes=64)
        w_plane = keep.tile([P, U_GROUPS, LATENT_GROUPS, SLOTS, P], U8, name="w_plane", align_bytes=64)
        y_plane = keep.tile([P, CHANNEL_GROUPS, M], U8, name="y_plane", align_bytes=64)
        warm = keep.tile([P, 2], F32, name="warm")

        def load_points(key, src, first_point, tiles, group):
            view = src[first_point : first_point + tiles * P, group * GROUP : (group + 1) * GROUP]
            tile = landing_tile(key, [P, tiles, GROUP], BF16)
            nc.sync.dma_start(out=tile[:], in_=view.rearrange("(i p) c -> p i c", p=P))

        def load_d2(k):
            load_points(("d2", k), d2, k // U_GROUPS * POINTS, TILES, k % U_GROUPS)

        def load_base(j):
            b, g = Y_PIECES[j]
            load_points(("base", j), base, b * POINTS, TILES, g)

        def load_a(h):
            tile = landing_tile(("a", h), [P, SLOTS, GROUP], BF16)
            view = a[:, h * GROUP : (h + 1) * GROUP].rearrange("(p t) f -> p t f", t=SLOTS)
            nc.sync.dma_start(out=tile[:], in_=view)

        def load_w(pair):
            tile = landing_tile(("w", pair), [P, 2, 2 * F], U8)
            view = w_words[2 * pair : 2 * pair + 2].rearrange("g p n -> p g n")
            nc.sync.dma_start(out=tile[:].bitcast(I32), in_=view.bitcast(I32))

        def load_w_scales():
            for q in range(4):
                nc.sync.dma_start(
                    out=loaded["w_scales"][32 * q : 32 * q + 4].bitcast(I32),
                    in_=w_scales[:, 4 * q : 4 * q + 4, :].rearrange("g r n -> r g n").bitcast(I32),
                )

        def load_v(h):
            loaded["v", h] = keep.tile([P, SLOTS, N], BF16, name="v_rows%d" % h)
            view = v[h * GROUP : (h + 1) * GROUP, :].rearrange("(r t e) n -> e r t n", t=SLOTS, e=4)
            for e in range(4):
                nc.sync.dma_start(out=loaded["v", h][e:P:4], in_=view[e])

        def load_columns(name, vec, groups):
            loaded[name] = keep.tile([P, groups, SLOTS], BF16, name=name)
            nc.sync.dma_start(out=loaded[name][:], in_=vec.rearrange("(g p t) -> p g t", p=P, t=SLOTS))

        def load_amp():
            loaded["amp"] = keep.tile([LATENT_GROUPS * SLOTS, P], BF16, name="amp_rows")
            for h in range(LATENT_GROUPS):
                nc.sync.dma_start(
                    out=loaded["amp"][SLOTS * h : SLOTS * (h + 1)].rearrange("t (r e) -> t r e", e=4),
                    in_=amp[h * GROUP : (h + 1) * GROUP].rearrange("(r t e) -> t r e", t=SLOTS, e=4),
                )

        def deal_w(pair):
            src = loaded["w", pair][:].bitcast(I32).rearrange("p g (h r t w) -> p (g h) t r w", h=2, t=SLOTS, w=2)
            dst = w_codes[:, 2 * pair : 2 * pair + 2].bitcast(I32).rearrange("p g h t (r w) -> p (g h) t r w", w=2)
            vector_copy(out=dst, in_=src)

        def deal_w_scales():
            src = loaded["w_scales"][:].bitcast(I32).rearrange("p g (h r t) -> p (g h) r t", h=2, t=SLOTS)
            vector_copy(out=w_plane[:].bitcast(I32).rearrange("p g h t r -> p (g h) r t"), in_=src)

        def pack_a(h, runs, copy):
            dst = packed_tile(("a", h), False)[:].rearrange("p (t r e) s -> p r t s e", t=SLOTS, e=4)
            src = loaded["a", h][:].rearrange("p s (r t e) -> p r t s e", t=SLOTS, e=4)
            copy(out=dst[:, runs], in_=src[:, runs])

        def pack_v(h, g, columns, copy):
            dst = packed_tile(("v", h, g), False)[:].rearrange("p (t q) s -> p q s t", t=SLOTS)
            src = loaded["v", h][:, :, g * GROUP : (g + 1) * GROUP].rearrange("p s (q t) -> p q s t", t=SLOTS)
            copy(out=dst[:, columns], in_=src[:, columns])

        def turn_amp(i):
            vector_copy(out=amp_square[0 : LATENT_GROUPS * SLOTS], in_=loaded["amp"][:])
            banks["amp"] = bank(i)
            nc.tensor.transpose(banks["amp"][:, 0:P], amp_square[:], ident[:])

        def channel_constants():
            vector_copy(out=spread_cols[:], in_=loaded["spread"][:])
            nc.vector.tensor_tensor(out=shift_cols[:], in0=loaded["bias"][:], in1=loaded["spread"][:], op=ALU.mult)

        def turn_words(dst, key, i, u):
            nc.tensor.transpose(dst, loaded[key][:].bitcast(F32)[:, i, u : GROUP // 2 : 2], ident[:])

        def turn_pairs(key, u, into):
            banks[key, u] = into
            for i in range(TILES):
                turn_words(into[:, i * P : (i + 1) * P], key, i, u)

        def slot_of(key, t):
            return banks[key, t // 2][:].bitcast(BF16)[:, t % 2 : 2 * POINTS : 2]

        def turn_x(b, half, into):
            banks[("x", b), half] = into
            for i in range(2):
                for u in range(2):
                    turn_words(into[:, (2 * i + u) * P : (2 * i + u + 1) * P], ("x", b), 2 * half + i, u)

        def pack_x(b):
            words = packed_tile(("x", b), False)[:].rearrange("p m t -> p (m t)").bitcast(F32)
            for half in range(2):
                scalar_copy(
                    out=words[:, half * POINTS : (half + 1) * POINTS].rearrange("p (i m u) -> p i m u", i=2, u=2),
                    in_=banks[("x", b), half][:].rearrange("p (i u m) -> p i m u", i=2, u=2),
                )

        def pack(key, points, copy, shared=True):
            copy(
                out=packed_tile(key, shared)[:, points, :].rearrange("p (c i) t -> p c t i", i=4),
                in_=rows[key][:, :, points].rearrange("p t (c i) -> p c t i", i=4),
            )

        def pack_on_gpsimd(key, points):
            nc.gpsimd.tensor_scalar(
                out=packed_tile(key, True)[:, points, :],
                in0=rows[key][:, :, points].rearrange("p t m -> p m t"),
                scalar1=1.0,
                scalar2=0.0,
                op0=ALU.mult,
                op1=ALU.add,
            )

        def log_d2(k):
            rows["log", k] = work.tile([P, SLOTS, POINTS], F32, name="scalar_rows", tag="scalar_rows")
            for u in range(2):
                src = banks[("d2", k), u][:].bitcast(BF16).rearrange("p (m e) -> p e m", e=2)
                nc.scalar.activation(out=rows["log", k][:, 2 * u : 2 * u + 2, :], in_=src, func=FUNC.Ln)

        def u_values(k):
            rows["u", k] = work.tile([P, SLOTS, POINTS], BF16, name="u_rows", tag="u_rows")
            for t in range(SLOTS):
                nc.vector.scalar_tensor_tensor(
                    out=rows["u", k][:, t, :],
                    in0=slot_of(("d2", k), t),
                    scalar=loaded["influence"][:, k % U_GROUPS, t : t + 1],
                    in1=rows["log", k][:, t, :],
                    op0=ALU.mult,
                    op1=ALU.mult,
                )

        def s_pass(b, h, t, step):
            if step == 0:
                codes, scales = mx["a", h]
                columns = slice(t * P, (t + 1) * P)
                weight, weight_scales, moving = codes[:, columns].bitcast(FP8X4), scales[:, columns], ("x", b)
            else:
                g = step - 1
                weight, weight_scales = w_codes[:, g, h, t, :].bitcast(FP4X4), w_plane[:, g, h, t, :]
                moving = ("u", U_GROUPS * b + g)
            mx_pass(banks["s", b, h, t][:], weight, weight_scales, moving, slice(None), step == 0, step == U_GROUPS)

        def s_by_bank(b, h, slots):
            for t in slots:
                banks["s", b, h, t] = next_bank()
                for step in range(U_GROUPS + 1):
                    s_pass(b, h, t, step)

        def s_by_pass(b, h, steps):
            for step in steps:
                for t in range(SLOTS):
                    s_pass(b, h, t, step)

        def tanh_s(b, h):
            rows["tanh", b, h] = work.tile([P, SLOTS, POINTS], F32, name="scalar_rows", tag="scalar_rows")
            for t in range(SLOTS):
                nc.scalar.activation(out=rows["tanh", b, h][:, t, :], in_=banks["s", b, h, t][:], func=FUNC.Tanh)

        def h_values(b, h, shared=False):
            gains = amp_cols[:, SLOTS * h : SLOTS * (h + 1)].unsqueeze(1).unsqueeze(3)
            nc.vector.tensor_tensor(
                out=packed_tile(("h", b, h), shared)[:].rearrange("p (c i) t -> p c t i", i=4),
                in0=rows["tanh", b, h][:].rearrange("p t (c i) -> p c t i", i=4),
                in1=gains.broadcast_to([P, POINTS // 4, SLOTS, 4]),
                op=ALU.mult,
            )

        def base_term(j, slots):
            g = Y_PIECES[j][1]
            if ("base", j) not in rows:
                rows["base", j] = work.tile([P, SLOTS, POINTS], F32, name="base_rows", tag="base_rows")
            for t in slots:
                nc.scalar.activation(
                    out=rows["base", j][:, t, :],
                    in_=slot_of(("base", j), t),
                    func=FUNC.Identity,
                    scale=spread_cols[:, g, t : t + 1],
                    bias=shift_cols[:, g, t : t + 1],
                )

        def y_product(j, t, points, out):
            b, g = Y_PIECES[j]
            banks["y", j, t, points.start] = out
            columns = slice(t * P, (t + 1) * P)
            for h in range(LATENT_GROUPS):
                codes, scales = mx["v", h, g]
                weight = codes[:, columns].bitcast(FP8X4)
                mx_pass(out, weight, scales[:, columns], ("h", b, h), points, h == 0, h == LATENT_GROUPS - 1)

        def y_values(j, slots, points):
            g = Y_PIECES[j][1]
            if ("y", j) not in rows:
                rows["y", j] = work.tile([P, SLOTS, POINTS], F32, name="y_rows", tag="y_rows")
            for t in slots:
                nc.vector.scalar_tensor_tensor(
                    out=rows["y", j][:, t, points],
                    in0=banks["y", j, t, points.start],
                    scalar=spread_cols[:, g, t : t + 1],
                    in1=rows["base", j][:, t, points],
                    op0=ALU.mult,
                    op1=ALU.add,
                )

        def turn_y(j, tiles):
            for i in tiles:
                banks["turned", j, i] = next_bank()
                for t in range(SLOTS):
                    nc.tensor.transpose(
                        banks["turned", j, i][:, t * P : (t + 1) * P], rows["y", j][:, t, i * P : (i + 1) * P], ident[:]
                    )

        def store_y(j, tiles):
            b, g = Y_PIECES[j]
            for i in tiles:
                out_tile = work.tile([P, P, SLOTS], F32, name="y_out", tag="y_out", bufs=6)
                scalar_copy(out=out_tile[:], in_=banks["turned", j, i][:].rearrange("m (t q) -> m q t", t=SLOTS))
                first = b * POINTS + i * P
                nc.sync.dma_start(
                    out=out_0[first : first + P, g * GROUP : (g + 1) * GROUP],
                    in_=out_tile[:].rearrange("m q t -> m (q t)"),
                )

        def quantize_y(j):
            b, g = Y_PIECES[j]
            mx["y", j] = work.tile([P, POINTS], U32, name="y_codes", tag="y_codes", bufs=3, align_bytes=64)
            nc.vector.quantize_mx(
                out=mx["y", j][:].bitcast(FP8X4),
                scales=y_plane[:, g, b * POINTS : (b + 1) * POINTS],
                in_=packed["y", j][:].rearrange("p m t -> p (m t)"),
            )

        def store_codes(j):
            b, g = Y_PIECES[j]
            dst = out_1[g, :, b * POINTS : (b + 1) * POINTS, :].rearrange("p m t -> p (m t)")
            nc.sync.dma_start(out=dst.bitcast(I32), in_=mx["y", j][:].bitcast(I32))

        def store_scales():
            for q in range(4):
                nc.sync.dma_start(
                    out=out_2[:, 4 * q : 4 * q + 4, :].rearrange("g r m -> r g m").bitcast(I32),
                    in_=y_plane[32 * q : 32 * q + 4].bitcast(I32),
                )

        everything = slice(0, POINTS)
        all_columns = slice(0, P)

        nc.vector.memset(warm[:], 1.0)
        nc.scalar.activation(out=warm[:, 1:2], in_=warm[:, 0:1], func=FUNC.Ln)
        make_identity(nc, ident[:])
        nc.gpsimd.memset(landing_tile("w_scales", [P, U_GROUPS, F], U8)[:].bitcast(I32), 0)
        nc.gpsimd.memset(amp_square[:], 0.0)
        for half in range(2):
            load_points(("d2", 0, half), d2, half * HALF, 2, 0)
        load_a(0)
        load_columns("influence", influence, U_GROUPS)
        load_d2(1)
        load_d2(2)
        load_points(("x", 0), x, 0, TILES, 0)
        load_d2(3)
        load_w_scales()
        load_amp()
        for u in range(2):
            banks[("d2", 0), u] = bank(u)
        for half in range(2):
            for u in range(2):
                for i in range(2):
                    column = (2 * half + i) * P
                    turn_words(banks[("d2", 0), u][:, column : column + P], ("d2", 0, half), i, u)
        pack_a(0, slice(0, 32), vector_copy)
        load_points(("x", 1), x, POINTS, TILES, 0)
        load_w(0)
        load_d2(4)
        load_w(1)
        load_d2(5)
        load_a(1)
        load_d2(6)

        def round_0():
            load_d2(7)
            load_columns("spread", spread, CHANNEL_GROUPS)
            load_columns("bias", bias, CHANNEL_GROUPS)
            load_v(1)
            load_v(0)

        def round_2():
            pack_x(0)
            quantize("a", 0)
            deal_w_scales()

        def round_3():
            pack_x(1)
            turn_amp(4)
            quantize("x", 0)
            deal_w(0)

        def round_7():
            channel_constants()
            quantize("x", 1)

        on_the_side = {
            0: round_0,
            2: round_2,
            3: round_3,
            4: lambda: deal_w(1),
            5: lambda: pack_a(1, slice(16, 32), vector_copy),
            6: lambda: quantize("a", 1),
            7: round_7,
        }
        last_u = U_PIECES - 1
        for k in range(U_PIECES):
            if k < last_u:
                for u in range(2):
                    turn_pairs(("d2", k + 1), u, bank(2 * ((k + 1) % 2) + u))
            if k in (1, 2):
                for half in range(2):
                    turn_x(k - 1, half, bank(2 + 2 * k + half))
            log_d2(k)
            if k in on_the_side:
                on_the_side[k]()
            if k > 1:
                quantize("u", k - 2)
            if k == 4:
                for t in range(SLOTS):
                    banks["s", 0, 0, t] = bank(4 + t)
                s_by_pass(0, 0, range(3))
            if k == 5:
                s_by_pass(0, 0, range(3, 5))
            if k == last_u:
                s_by_bank(0, 1, range(2))
            if k > 0:
                pack_on_gpsimd(("u", k - 1), slice(U_REST, POINTS))
            if 0 < k < last_u:
                pack(("u", k - 1), slice(0, U_REST), scalar_copy)
            u_values(k)
            if k == last_u:
                pack(("u", k - 1), slice(0, U_REST), vector_copy)
            if k == 3:
                vector_copy(out=amp_cols[:], in_=banks["amp"][:, 0 : LATENT_GROUPS * SLOTS])
            if k == 4:
                pack_a(1, slice(0, 16), scalar_copy)
            if k >= 2:
                load_base(k - 2)

        tanh_s(0, 0)
        quantize("u", last_u - 1)
        pack(("u", last_u), everything, vector_copy)
        s_by_bank(0, 1, range(2, 4))
        for t in range(SLOTS):
            banks["s", 1, 0, t] = next_bank()
        s_by_pass(1, 0, range(U_GROUPS))
        h_values(0, 0)
        quantize("u", last_u)
        s_by_pass(1, 0, range(U_GROUPS, U_GROUPS + 1))
        tanh_s(0, 1)
        pack_v(1, 0, all_columns, vector_copy)
        quantize("h", 0, 0)
        pack_v(0, 0, all_columns, scalar_copy)
        for u in range(2):
            turn_pairs(("base", 0), u, next_bank())
        tanh_s(1, 0)
        base_term(0, range(SLOTS))
        h_values(0, 1)
        quantize("v", 1, 0)
        quantize("h", 0, 1)
        quantize("v", 0, 0)
        s_by_bank(1, 1, range(SLOTS))
        h_values(1, 0)
        pack_v(0, 1, all_columns, scalar_copy)
        pack_v(1, 1, all_columns, vector_copy)
        quantize("h", 1, 0)
        quantize("v", 1, 1)
        tanh_s(1, 1)
        quantize("v", 0, 1)

        def product_half(j, half):
            for t in (2 * half, 2 * half + 1):
                y_product(j, t, everything, next_bank()[:])

        def turn_half(j, half):
            if j > 0:
                turn_y(j - 1, (2 * half, 2 * half + 1))
            turn_pairs(("base", j + 1), half, next_bank())

        def take_half(j, half):
            if j > 0:
                store_y(j - 1, (2 * half, 2 * half + 1))
            base_term(j + 1, (2 * half, 2 * half + 1))

        last_y = len(Y_PIECES) - 1
        for j in range(last_y):
            product_half(j, 0)
            turn_half(j, 0)
            product_half(j, 1)
            if j == 1:
                h_values(1, 1, shared=True)
                quantize("h", 1, 1)
            if j > 1:
                pack(("y", j - 2), slice(0, Y_REST), vector_copy)
            if j == 2:
                pack_v(1, 2, all_columns, vector_copy)
            if j == 3:
                quantize("v", 0, 2)
                quantize("v", 1, 2)
            if j > 1:
                quantize_y(j - 2)
                store_codes(j - 2)
            if 0 < j < last_y - 1:
                pack_on_gpsimd(("y", j - 1), slice(Y_REST, POINTS))
            if j == last_y - 1:
                pack(("y", j - 1), everything, vector_copy)
            y_values(j, range(2), everything)
            if j == last_y - 1:
                quantize_y(j - 1)
            y_values(j, range(2, 4), everything)
            take_half(j, 0)
            if j == last_y - 1:
                store_codes(j - 1)
            turn_half(j, 1)
            take_half(j, 1)
            if j < 2:
                pack_v(0, 2, slice(j * P // 2, (j + 1) * P // 2), scalar_copy)

        halves = [slice(0, HALF), slice(HALF, POINTS)]

        def last_product(points):
            for pair in range(2):
                both = next_bank()
                for e in range(2):
                    y_product(last_y, 2 * pair + e, points, both[:, e * HALF : (e + 1) * HALF])

        last_product(halves[0])
        turn_y(last_y - 1, range(TILES))
        last_product(halves[1])
        pack(("y", last_y - 1), everything, vector_copy)
        y_values(last_y, range(SLOTS), halves[0])
        quantize_y(last_y - 1)
        store_y(last_y - 1, range(2))
        store_codes(last_y - 1)
        store_y(last_y - 1, range(2, TILES))
        y_values(last_y, range(SLOTS), halves[1])
        turn_y(last_y, range(TILES))
        pack(("y", last_y), everything, vector_copy)
        quantize_y(last_y)
        store_y(last_y, range(3))
        store_codes(last_y)
        store_y(last_y, range(3, TILES))
        store_scales()
